import numpy as np, ml_dtypes
CORES = [5,29,101,125,133,157,229,253]
N = 8
import mx_ref
BF = ml_dtypes.bfloat16
def entries(a):
    return np.ascontiguousarray(a.T).reshape(-1)
def table(e):
    return np.ascontiguousarray(np.reshape(e, (-1, 16)).T).astype(np.int32)
def pick(q, e):
    c = np.concatenate([q[0].reshape(128, -1, 4), np.zeros((128, 1, 4), np.uint8)], axis=1); s = np.concatenate([q[1], np.ones((16, 1), np.uint8)], axis=1)
    return (np.ascontiguousarray(c[:, e].reshape(128, -1)), np.ascontiguousarray(s[:, e]))
def join(*qs):
    return (np.concatenate([q[0] for q in qs], axis=1), np.concatenate([q[1] for q in qs], axis=1))
def put(q, e, v):
    c, s = q[0].reshape(128, -1, 4).copy(), q[1].copy(); c[:, e] = v[0].reshape(128, -1, 4); s[:, e] = v[1]
    return (c.reshape(128, -1), s)
def pk(c, s):
    return (np.ascontiguousarray(c), mx_ref.live(s))
def emit(q):
    return q[0], q[1]
def packed(v, rng):
    q = [mx_ref.quantize(np.ascontiguousarray(v[r])) for r in range(N)]
    return np.stack([a for a, b in q]), np.stack([mx_ref.plane(b, rng) for a, b in q])
def cols(t, e):
    v = np.concatenate([t.reshape(128, -1, 4), np.zeros((128, 1, 4), BF)], axis=1)
    return np.ascontiguousarray(v[:, e]).reshape(128, -1)
def f(rng, *shape):
    return mx_ref.flush((rng.standard_normal(shape, dtype=np.float32) * np.exp2(rng.integers(-2, 3, shape[:-1] + (1,)))).astype(BF))
def wide(rng, *shape, cols=0):
    v = rng.standard_normal(shape, dtype=np.float32) * np.exp2(rng.integers(-12, 13, shape)).astype(np.float32)
    if cols: v *= np.repeat(np.exp2(rng.integers(-cols, cols + 1, shape[:-2] + (1, shape[-1] // 4))) * (rng.random(shape[:-2] + (1, shape[-1] // 4)) > 0.0625), 4, axis=-1).astype(np.float32)
    return mx_ref.flush(v.astype(BF))
T, C, CAPP, M = 128, 512, 16, 64
def first(v):
    z = np.zeros((N, 128, 512), BF); z[:, :, :4] = v; return z
def lists(rng, full=False, one=False, odd=False):
    h = int(rng.integers(0, N)); a = rng.permutation(np.delete(np.arange(N), h))
    sn = np.full((N, N, CAPP), -1)
    for d in range(N):
        m, o = int(rng.integers(1, M + 1)), rng.permutation(N * CAPP)
        if odd: m = 2 * int(rng.integers(0, M // 2)) + 1
        if full:
            w = np.isin(o // CAPP, a[:M // CAPP] if d == h else a[:1]); o = np.concatenate([o[w], o[~w]])
            m = M if d == h else int(rng.integers(CAPP, M + 1))
        if one: o = o[o // CAPP != a[0]]
        if one and d == h: m, o = 1, o[o // CAPP != h]
        o = o[:m]
        sn[o // CAPP, d, o % CAPP] = rng.integers(0, T, m)
    return np.stack([table(sn[s]) for s in range(N)])
def setup_inputs(rng):
    kc, ks = packed(f(rng, N, 128, 4 * C), rng)
    return {"x": f(rng, N, 128, 4 * T), "u": first(f(rng, N, 128, 4)), "w": f(rng, N, 128, 512), "kc": kc, "ks": ks, "sn": lists(rng)}
def setup_inputs_full(rng):
    return {**setup_inputs(rng), "sn": lists(rng, full=True)}
def setup_inputs_high(rng):
    d = setup_inputs(rng); g = np.where(rng.permutation(N) < N // 2, 1, -1).astype(np.float32)[:, None, None]
    p = rng.permutation(N)
    g = g * np.where(p < N // 2, 2.0 ** 24, 2.0 ** -24).astype(np.float32)[:, None, None]
    k = np.where(p == N - 1, 2.0 ** -24, 2.0 ** 24).astype(np.float32)[:, None, None]
    d["u"] = first(((np.abs(f(rng, N, 128, 4).astype(np.float32)) + 1) * k).astype(BF))
    d["kc"], d["ks"] = packed((g * (1 + np.abs(f(rng, N, 128, 4 * C).astype(np.float32)))).astype(BF), rng); return d
def setup_inputs_one(rng):
    return {**setup_inputs(rng), "sn": lists(rng, one=True)}
def setup_inputs_spread(rng):
    d = setup_inputs(rng); d["x"] = wide(rng, N, 128, 4 * T, cols=8)
    d["kc"], d["ks"] = packed(wide(rng, N, 128, 4 * C, cols=8), rng); return d
def setup_inputs_ties(rng):
    d = setup_inputs(rng); v = f(rng, N, 128, C // 8 * 4)
    d["kc"], d["ks"] = packed(np.stack([cols(v[r], rng.permutation(np.arange(C) // 8)) for r in range(N)]), rng)
    d["u"][int(rng.integers(0, N))] = 0
    d["sn"] = lists(rng, odd=True); return d
def scores(u, kc, ks):
    return mx_ref.matmul(mx_ref.quantize(np.ascontiguousarray(u)), pk(kc, ks))[0] + np.float32(0)
def check_inputs(d):
    b = []
    for r in range(N):
        if (d["u"][r][:, 4:].astype(np.float32) != 0).any(): b.append("u")
        e = entries(d["sn"][r])
        m = sum(int((entries(d["sn"][s])[r * CAPP:r * CAPP + CAPP] >= 0).sum()) for s in range(N))
        if e.min() < -1 or e.max() >= T or m < 1 or m > M: b.append("sn")
        try: good = bool(np.isfinite(scores(d["u"][r], d["kc"][r], d["ks"][r])).all())
        except Exception: good = False
        if not good: b.append("kc")
    return b
def reference(x, u, w, kc, ks, sn):
    oc, osc, ev = np.zeros((N, 128, 4 * C), np.uint8), np.zeros((N, 16, C), np.uint8), np.zeros((N, 2, M), np.float32)
    y = np.zeros((N, 128, C), np.float32)
    new = join(*[mx_ref.quantize(np.ascontiguousarray(x[s])) for s in range(N)])
    for d in range(N):
        e = []
        for s in range(N):
            v = entries(sn[s])[d * CAPP:d * CAPP + CAPP]; e.append(s * T + v[v >= 0])
        e = np.concatenate(e); m = e.size
        z = scores(u[d], kc[d], ks[d])
        out = np.argsort(z, kind="stable")[:m]
        after = put(pk(kc[d], ks[d]), out, pick(new, e))
        oc[d], osc[d] = emit(after)
        ev[d, 0] = -1; ev[d, 0, :m] = out; ev[d, 1, :m] = z[out]
        y[d] = mx_ref.matmul(mx_ref.quantize(np.ascontiguousarray(w[d])), after)
    return {"oc": oc, "osc": osc, "ev": ev, "y": y}

@@ -1,0 +1,363 @@
+from concourse.bass import DstId, RemoteDMATransfer
+from concourse.mybir import dt, AluOpType as A, AxisListType, ActivationFunctionType as F
+
+CODES, PLANE = "float8_e4m3fn_x4", "uint8"
+BIG = 1.0e29
+SCRATCH = {
+    "snr": ("sbuf", [128, 8], "int32"),
+    "xt": ("sbuf", [128, 520], "bfloat16"),
+    "ut": ("sbuf", [128, 512], "bfloat16"),
+    "wt": ("sbuf", [128, 512], "bfloat16"),
+    "xq": ("sbuf", [128, 130], CODES), "xs": ("sbuf", [128, 130], PLANE),
+    "uq": ("sbuf", [128, 128], CODES), "us": ("sbuf", [128, 128], PLANE),
+    "ur": ("sbuf", [128, 128], CODES), "urs": ("sbuf", [128, 128], PLANE),
+    "wq": ("sbuf", [128, 128], CODES), "ws": ("sbuf", [128, 128], PLANE),
+    "kq": ("sbuf", [128, 576], CODES), "kp": ("sbuf", [128, 576], PLANE),
+    "pq": ("sbuf", [128, 128], CODES), "ps": ("sbuf", [128, 128], PLANE),
+    "fwl": ("sbuf", [128, 2], "uint16"),
+    "fwq": ("sbuf", [128, 32], CODES), "fws": ("sbuf", [128, 32], PLANE),
+    "rl": ("sbuf", [128, 8], "uint16"),
+    "lq": ("sbuf", [128, 128], CODES), "ls": ("sbuf", [128, 128], PLANE),
+    "oq": ("sbuf", [128, 512], CODES), "os_": ("sbuf", [128, 512], PLANE),
+    "lst": ("sbuf", [128, 8], "uint16"), "lo": ("sbuf", [128, 2], "uint16"),
+    "zo": ("sbuf", [128, 8], "uint16"), "coff": ("sbuf", [128, 4], "uint16"),
+    "loff": ("sbuf", [128, 32], "uint16"), "roff": ("sbuf", [128, 32], "uint16"),
+    "pi": ("sbuf", [128, 1], "int32"), "pm": ("sbuf", [128, 1], "int32"), "pmf": ("sbuf", [128, 1], "float32"),
+    "q16": ("sbuf", [128, 32], "float32"), "jw": ("sbuf", [128, 32], "float32"), "jm": ("sbuf", [128, 32], "float32"),
+    "kb": ("sbuf", [128, 4], "float32"), "ft": ("sbuf", [128, 136], "float32"), "zr": ("sbuf", [128, 128], "float32"),
+    "neg": ("sbuf", [128, 512], "float32"), "mk": ("sbuf", [128, 512], "float32"),
+    "k64": ("sbuf", [128, 64], "float32"), "acol": ("sbuf", [128, 4], "float32"),
+    "sm": ("sbuf", [128, 512], "float32"),
+    "c0": ("sbuf", [128, 640], "bfloat16"), "c1": ("sbuf", [128, 640], "bfloat16"),
+    "c2": ("sbuf", [128, 640], "bfloat16"), "c3": ("sbuf", [128, 640], "bfloat16"),
+    "junk": ("sbuf", [128, 640], "bfloat16"), "scn": ("sbuf", [128, 320], "float32"),
+    "tin": ("sbuf", [128, 128], "float32"), "tt": ("sbuf", [128, 128], "float32"),
+    "rin": ("sbuf", [128, 32], "float32"), "rwp": ("sbuf", [128, 32], "float32"), "rw": ("sbuf", [128, 32], "float32"),
+    "dd": ("sbuf", [128, 32], "float32"), "lm": ("sbuf", [128, 32], "float32"), "lt": ("sbuf", [128, 32], "float32"),
+    "fl": ("sbuf", [128, 128], "float32"), "pinc": ("sbuf", [128, 128], "float32"), "zq": ("sbuf", [128, 4], "float32"),
+    "m64": ("sbuf", [128, 64], "float32"),
+    "evin": ("sbuf", [128, 512], "float32"), "evs": ("sbuf", [128, 512], "float32"),
+    "e1": ("sbuf", [128, 64], "float32"), "e2": ("sbuf", [128, 64], "float32"), "e3": ("sbuf", [128, 64], "float32"),
+    "yb": ("sbuf", [128, 512], "float32"),
+    "pr": ("psum", [128, 512], "float32"), "pc": ("psum", [128, 2048], "float32"),
+    "p2": ("psum", [128, 512], "float32"), "py": ("psum", [128, 1024], "float32"),
+}
+SEMAPHORES = ["sv", "ss", "st", "sg", "dsn", "dx", "du", "dk", "dw", "down", "dr", "dout",
+              "aL", "aC", "aS", "fL", "fC", "fS", "loc"]
+KINDS = ("L", "C", "S")
+
+
+def bits(es):
+    m = 0
+    for e in es:
+        m |= 1 << e
+    return m
+
+
+def plan(s, T, topo):
+    core = T.cores[s]
+    n = len(T.cores)
+    cross = [d for d in range(n) if d != s and not topo.may_write(core, T.cores[d])]
+    home = [d for d in range(n) if d not in cross]
+    same = [d for d in home if d != s]
+    ports = [f for f in topo.cores_of(core) if f != core and all(topo.may_write(f, T.cores[d]) for d in cross)]
+    near = [f for f in ports if topo.die(f) == topo.die(core)][0]
+    far = [f for f in ports if topo.die(f) != topo.die(core)][0]
+    fw = [near, far] if (s // 2) % 2 == 0 else [far, near]
+    off = topo.engines(core, T.cores[same[0]])
+    on = [e for e in topo.engines(core, near) if e not in off]
+    h = len(on) // 2
+    hop = [(fw[0], on[:h], cross[:2]), (fw[1], on[h:], cross[2:])]
+    q = len(off) // 4
+    parts = {"L": (off[:2 * q], off[2 * q:3 * q], off[3 * q:]),
+             "C": (off[:2 * q], off[2 * q:3 * q], off[3 * q:]),
+             "S": (off[2 * q:], off[:q], off[q:2 * q])}
+    return {"core": core, "cross": cross, "home": home, "same": same, "hop": hop, "parts": parts}
+
+
+def onward(f, dst, i, topo):
+    es = topo.engines(f, dst)
+    h = len(es) // 2
+    return es[:h] if i == 0 else es[h:]
+
+
+def xfer(src_core, dst_core, es, sem, src, dst, topo):
+    rid, pid = topo.addr(dst_core, src_core)
+    return RemoteDMATransfer(dst_ids=[DstId(rid=rid, pnc=pid)], dma_engine_mask=bits(es), remote_sem=sem, srcs=[src], dsts=[dst])
+
+
+def u8(v):
+    return v.bitcast(dt.uint8)
+
+
+def u32(v):
+    return v.bitcast(dt.uint32)
+
+
+def forward(g, core, s, T, topo):
+    p = plan(s, T, topo)
+    loc = 0
+    for f, es, ds in p["hop"]:
+        if f != core:
+            continue
+        for k in KINDS:
+            g.wait_ge(T.sem["f" + k], len(es))
+            ts = []
+            for i, d in enumerate(ds):
+                dc = T.cores[d]
+                me = onward(core, dc, i, topo)
+                if k == "L":
+                    a, b = T.fwl[:, i:i + 1], T.rl[:, s:s + 1]
+                elif k == "C":
+                    a, b = u8(T.fwq[:, 16 * i:16 * i + 16]), u8(T.lq[:, 16 * s:16 * s + 16])
+                else:
+                    a, b = T.fws[:, 16 * i:16 * i + 16], T.ls[:, 16 * s:16 * s + 16]
+                ts.append(xfer(core, dc, me, T.sem["a" + k], a, b, topo))
+                loc += len(me)
+            g.remote_dma_fused(ts, local_sem=T.sem.loc)
+        g.wait_ge(T.sem.loc, loc)
+
+
+def rank_program(g, core, T, topo):
+    r = T.rank_of(core)
+    if r is None:
+        for s in range(len(T.cores)):
+            if T.cores[s] in topo.cores_of(core):
+                forward(g, core, s, T, topo)
+        return
+    n = len(T.cores)
+    P = plan(r, T, topo)
+    V, S, E, Y = g.vector, g.scalar, g.tensor, g.sync
+    sem = T.sem
+    cnt = {"v": 0, "s": 0, "t": 0, "g": 0}
+    seen = {}
+
+    def done(q, inst):
+        inst.then_inc(sem["s" + q], 1)
+        cnt[q] += 1
+        return ("s" + q, cnt[q])
+
+    def w(name, queue, *tags):
+        for sn, v in tags:
+            if seen.get((name, sn), 0) < v:
+                queue.wait_ge(sem[sn], v)
+                seen[(name, sn)] = v
+
+    def v(call, *tags):
+        w("v", V, *tags)
+        return done("v", call())
+
+    def sc(call, *tags):
+        w("s", S, *tags)
+        return done("s", call())
+
+    def mm(call, *tags):
+        w("t", E, *tags)
+        return done("t", call())
+
+    def gg(call, *tags):
+        w("g", g, *tags)
+        return done("g", call())
+
+    need = {"L": 0, "C": 0, "S": 0}
+    for s in range(n):
+        if s == r:
+            continue
+        p = plan(s, T, topo)
+        for k in KINDS:
+            for f, es, ds in p["hop"]:
+                if r in ds:
+                    need[k] += len(onward(f, core, ds.index(r), topo))
+            if r in p["same"]:
+                need[k] += len(p["parts"][k][p["same"].index(r)])
+
+    for k in range(4):
+        Y.dma_start(T.snr[16 * k:16 * k + 16, :], T.sn[:, :]).then_inc(sem.dsn, 16)
+        S.dma_start(T.snr[64 + 16 * k:80 + 16 * k, :], T.sn[:, :]).then_inc(sem.dsn, 16)
+    Y.dma_start(T.xt[:, 8:520], T.x[:, :]).then_inc(sem.dx, 16)
+    S.dma_start(T.ut[:, 0:8], T.u[:, 0:8]).then_inc(sem.du, 16)
+    S.dma_start(u8(T.kq[:, 0:512]), T.kc[:, :]).then_inc(sem.dk, 16)
+    Y.dma_start(T.kp[:, 0:512], T.ks[:, :]).then_inc(sem.dk, 16)
+    Y.dma_start(T.wt[:, :], T.w[:, :]).then_inc(sem.dw, 16)
+    SN, DX, DU, DK, DW = ("dsn", 128), ("dx", 16), ("du", 16), ("dk", 32), ("dw", 16)
+
+    a_neg = v(lambda: V.memset(T.neg[:, :], -BIG))
+    a_x0 = v(lambda: V.memset(T.xt[:, 0:8], 0.0))
+    a_u0 = v(lambda: V.memset(T.ut[:, 8:512], 0.0))
+    a_zo = v(lambda: V.memset(T.zo[:, :], 0))
+    a_pi = gg(lambda: g.iota(T.pi[:, :], [[1, 1]], 0, 1))
+    a_q16 = gg(lambda: g.iota(T.q16[:, :], [[16, 32]], 0, 0, allow_small_or_imprecise_dtypes=True))
+    a_mk = gg(lambda: g.affine_select(T.mk[:, :], T.neg[:, :], [[0, 4], [-1, 128]], A.is_gt, BIG, 0, 1), a_neg)
+    a_ft = v(lambda: V.memset(T.ft[:, 2:136], 1.0))
+    a_ft = v(lambda: V.memset(T.ft[:, 0:2], 0.0))
+    v(lambda: V.memset(T.zr[:, :], 0.0))
+    v(lambda: V.memset(T.tin[:, :], 0.0))
+    v(lambda: V.memset(T.evin[32:64, :], 0.0))
+    t = v(lambda: V.memset(T.acol[:, :], 0.0))
+    a_con = v(lambda: V.memset(T.acol[0:32, :], 1.0), t)
+
+    cx, hm = P["cross"], P["home"]
+    stx, sth = cx[1] - cx[0], hm[1] - hm[0]
+    a_lx = v(lambda: V.tensor_scalar(T.lst[:, 0:4], T.snr[:, cx[0]:cx[0] + 3 * stx + 1:stx], 2, None, A.add), SN)
+    a_ly = v(lambda: V.tensor_scalar(T.lst[:, 4:8], T.snr[:, hm[0]:hm[0] + 3 * sth + 1:sth], 2, None, A.add))
+    a_lo = v(lambda: V.tensor_scalar(T.lo[:, 0:1], T.snr[:, r:r + 1], 2, None, A.add))
+    a_xq = v(lambda: V.quantize_mx(T.xq[:, 0:130], T.xs[:, 0:130], T.xt[:, 0:520]), DX, a_x0)
+
+    def pick(o, os_, i, is_, b, off, lo, vt, st):
+        a, e = o
+        c, d = i
+        x = v(lambda: V.tensor_copy(u32(T[a][:, e[0]:e[1]]), u32(T[c][:, d[0]:d[1]]).indirect(T[off][:, lo[0]:lo[1]])), *vt)
+        y = sc(lambda: S.activation(T[os_][:, e[0]:e[1]], T[is_][:, d[0]:d[1]].indirect(T[off][:, lo[0]:lo[1]]), F.Copy), *st)
+        return x, y
+
+    X = ("xq", (0, 130))
+    pxc, pxs = pick(("pq", (0, 64)), "ps", X, "xs", None, "lst", (0, 4), (a_xq, a_lx), (a_xq, a_lx))
+    pyc, pys = pick(("pq", (64, 128)), "ps", X, "xs", None, "lst", (4, 8), (a_ly,), (a_ly,))
+    poc, pos = pick(("lq", (16 * r, 16 * r + 16)), "ls", X, "xs", None, "lo", (0, 1), (a_lo,), (a_lo,))
+    w("y", Y, a_lo)
+    Y.dma_start(T.rl[:, r:r + 1], T.lo[:, 0:1]).then_inc(sem.down, 16)
+
+    loc = 0
+
+    def hop1(k):
+        tot = 0
+        ts = []
+        for i, (f, es, ds) in enumerate(P["hop"]):
+            if k == "L":
+                a, b = T.lst[:, 2 * i:2 * i + 2], T.fwl[:, 0:2]
+            elif k == "C":
+                a, b = u8(T.pq[:, 32 * i:32 * i + 32]), u8(T.fwq[:, 0:32])
+            else:
+                a, b = T.ps[:, 32 * i:32 * i + 32], T.fws[:, 0:32]
+            ts.append(xfer(core, f, es, sem["f" + k], a, b, topo))
+            tot += len(es)
+        g.remote_dma_fused(ts, local_sem=sem.loc)
+        return tot
+
+    def straight(k):
+        tot = 0
+        ts = []
+        for i, d in enumerate(P["same"]):
+            es = P["parts"][k][i]
+            j = 4 + hm.index(d)
+            if k == "L":
+                a, b = T.lst[:, j:j + 1], T.rl[:, r:r + 1]
+            elif k == "C":
+                a, b = u8(T.pq[:, 16 * j:16 * j + 16]), u8(T.lq[:, 16 * r:16 * r + 16])
+            else:
+                a, b = T.ps[:, 16 * j:16 * j + 16], T.ls[:, 16 * r:16 * r + 16]
+            ts.append(xfer(core, T.cores[d], es, sem["a" + k], a, b, topo))
+            tot += len(es)
+        g.remote_dma_fused(ts, local_sem=sem.loc)
+        return tot
+
+    w("g", g, a_lx)
+    loc += hop1("L")
+    w("g", g, pxc)
+    loc += hop1("C")
+    w("g", g, pxs)
+    loc += hop1("S")
+    w("g", g, a_ly)
+    loc += straight("L")
+    w("g", g, pyc)
+    loc += straight("C")
+    w("g", g, pys)
+    loc += straight("S")
+    a_jr = gg(lambda: g.iota(T.evin[0:32, :], [[1, 512]], 0, 0, allow_small_or_imprecise_dtypes=True))
+    a_k64 = gg(lambda: g.iota(T.k64[:, :], [[1, 64]], 0, 0, allow_small_or_imprecise_dtypes=True))
+
+    a_uq = v(lambda: V.quantize_mx(T.uq[:, :], T.us[:, :], T.ut[:, :]), DU, a_u0)
+    urc, urs = pick(("ur", (0, 128)), "urs", ("uq", (0, 128)), "us", None, "zo", (0, 8), (a_uq, a_zo), (a_uq, a_zo))
+    a_row = mm(lambda: E.matmul_mx(T.pr[:, :], T.ur[:, :], T.urs[:, :], T.kq[:, 0:512], T.kp[:, 0:512], True, True), DK, urc, urs)
+    a_col = []
+    for c in range(4):
+        a_col.append(mm(lambda: E.matmul_mx(T.pc[:, 512 * c:512 * c + 128], T.kq[:, 128 * c:128 * c + 128],
+                                            T.kp[:, 128 * c:128 * c + 128], T.ur[:, :], T.urs[:, :], True, True)))
+    a_row2 = mm(lambda: E.matmul_mx(T.p2[:, :], T.ur[:, :], T.urs[:, :], T.kq[:, 0:512], T.kp[:, 0:512], True, True))
+    t = v(lambda: V.tensor_scalar(T.pm[:, :], T.pi[:, :], 15, None, A.bitwise_and), a_pi)
+    t = v(lambda: V.tensor_copy(T.pmf[:, :], T.pm[:, :]), t)
+    a_jw = v(lambda: V.tensor_scalar(T.jw[:, :], T.q16[:, :], T.pmf[:, 0:1], None, A.add), t, a_q16)
+    a_jm = v(lambda: V.tensor_scalar(T.jm[:, :], T.q16[:, :], T.pmf[:, 0:1], -512.0, A.add, A.add))
+    a_kb = v(lambda: V.tensor_scalar(T.kb[:, :], T.q16[:, 0:4], T.pmf[:, 0:1], 0.5, A.add, A.add))
+    a_wq = v(lambda: V.quantize_mx(T.wq[:, :], T.ws[:, :], T.wt[:, :]), DW)
+
+    a_sm = v(lambda: V.tensor_tensor(T.sm[:, :], T.pr[:, :], T.mk[:, :], A.max), a_row, a_mk)
+    sums = []
+    for c in range(4):
+        b = T["c%d" % c]
+        sj = T.pc[:, 512 * c:512 * c + 1]
+        if c:
+            v(lambda: V.tensor_scalar(b[:, 0:128 * c], T.pr[:, 0:128 * c], sj, None, A.is_le), a_col[c])
+        v(lambda: V.tensor_scalar(b[:, 128 * c:512], T.pr[:, 128 * c:512], sj, None, A.is_lt), a_col[c])
+        t = v(lambda: V.tensor_scalar(b[:, 512:640], T.sm[:, 128 * c:128 * c + 128], sj, None, A.is_equal), a_sm)
+        if c < 3:
+            sums.append(sc(lambda: S.activation(T.junk[:, :], b[:, :], F.Copy, accum_out=T.tin[:, 32 * c:32 * c + 1]), t, a_con,
+                           *sums[-1:]))
+        else:
+            t = v(lambda: V.tensor_tensor_scan(T.scn[:, :], b[:, 0:320], b[:, 320:640], 0.0, A.add, A.add), t)
+            sums.append(v(lambda: V.tensor_copy(T.tin[:, 32 * c:32 * c + 1], T.scn[:, 319:320]), t))
+    a_ev64 = sc(lambda: S.activation(T.evin[64:128, :], T.p2[64:128, :], F.Copy), a_row2)
+    a_tt = v(lambda: V.transpose(T.tt[:, :], T.tin[:, :]), *sums)
+    for a in range(4):
+        q, nm = (Y, "y") if a % 2 == 0 else (S, "s")
+        w(nm, q, a_tt)
+        q.dma_start(T.rin[32 * a:32 * a + 32, 0:16], T.tt[0:128:32, 0:128]).then_inc(sem.dr, 16)
+
+    a_fl = v(lambda: V.tensor_copy(T.fl[:, :], T.ft[:, 0:136].indirect(T.rl[:, 0:8])), ("aL", need["L"]), ("down", 16), a_ft)
+    a_pinc = v(lambda: V.tensor_tensor_scan(T.pinc[:, :], T.fl[:, :], T.zr[:, :], 0.0, A.add, A.add), a_fl)
+    m = T.pinc[:, 127:128]
+    for q in range(4):
+        a_z = sc(lambda: S.activation(T.junk[:, 0:127], T.pinc[:, 0:127], F.Sign, bias=T.kb[:, q:q + 1], scale=-1.0,
+                                      accum_out=T.zq[:, q:q + 1]), a_pinc, a_kb, sums[2] if q == 0 else a_z)
+    a_m64 = v(lambda: V.tensor_scalar(T.m64[:, :], T.k64[:, :], m, None, A.is_lt), a_pinc, a_k64)
+    t = v(lambda: V.tensor_copy(T.rin[:, 16:32], T.rin[:, 0:16]), ("dr", 64))
+    a_rwp = v(lambda: V.transpose(T.rwp[:, :], T.rin[:, :]), t)
+    for a in range(4):
+        for h in range(2):
+            a_rw = v(lambda: V.tensor_copy(T.rw[:, 2 * a + h:32:8], T.rwp[:, 8 * a + h:8 * a + 8:2]), a_rwp)
+    a_dd = v(lambda: V.tensor_tensor(T.dd[:, :], T.rw[:, :], T.jm[:, :], A.subtract), a_rw, a_jm)
+    a_lm = v(lambda: V.tensor_scalar(T.lm[:, :], T.rw[:, :], m, None, A.is_lt))
+    t = v(lambda: V.tensor_tensor(T.lt[:, :], T.dd[:, :], T.lm[:, :], A.mult), a_dd, a_lm)
+    a_loff = v(lambda: V.tensor_tensor(T.lt2[:, :] if False else T.dd[:, :], T.lt[:, :], T.jw[:, :], A.add), t, a_jw)
+    a_loff = v(lambda: V.tensor_copy(T.loff[:, :], T.dd[:, :]), a_loff)
+    a_roff = v(lambda: V.tensor_copy(T.roff[:, :], T.rw[:, :]), a_rw)
+    a_coff = v(lambda: V.tensor_scalar(T.coff[:, :], T.zq[:, :], 0.5, 63.5, A.mult, A.add), a_z)
+
+    cc, cs = pick(("kq", (512, 576)), "kp", ("lq", (0, 128)), "ls", None, "coff", (0, 4),
+                  (("aC", need["C"]), poc, a_coff), (("aS", need["S"]), pos, a_coff))
+    fin = []
+    for h in range(2):
+        x, y = pick(("oq", (256 * h, 256 * h + 256)), "os_", ("kq", (0, 576)), "kp", None, "loff", (16 * h, 16 * h + 16),
+                    (cc, a_loff), (cs, a_loff))
+        fin.append((x, y))
+    ym = []
+    for h in range(2):
+        lo, hi = 256 * h, 256 * h + 256
+        ym.append(mm(lambda: E.matmul_mx(T.py[:, 512 * h:512 * h + 256], T.wq[:, :], T.ws[:, :], T.oq[:, lo:hi], T.os_[:, lo:hi],
+                                         True, True), a_wq, *fin[h]))
+    yc = [sc(lambda: S.activation(T.yb[:, 0:256], T.py[:, 0:256], F.Copy), ym[0]),
+          v(lambda: V.tensor_copy(T.yb[:, 256:512], T.py[:, 512:768]), ym[1])]
+    outs = 0
+    for h in range(2):
+        w("y", Y, fin[h][0])
+        Y.dma_start(T.oc[:, 1024 * h:1024 * h + 1024], u8(T.oq[:, 256 * h:256 * h + 256])).then_inc(sem.dout, 16)
+        outs += 16
+    for h in range(2):
+        w("y", Y, yc[h])
+        Y.dma_start(T.y[:, 256 * h:256 * h + 256], T.yb[:, 256 * h:256 * h + 256]).then_inc(sem.dout, 16)
+        outs += 16
+        if h == 0:
+            w("y", Y, fin[1][1])
+            for k in range(4):
+                Y.dma_start(T.osc[4 * k:4 * k + 4, :], T.os_[32 * k:32 * k + 4, :]).then_inc(sem.dout, 16)
+                outs += 16
+
+    a_ev = v(lambda: V.tensor_copy(T.evs[:, 0:512].indirect(T.roff[:, 0:32]), T.evin[:, :]), a_roff, a_jr, a_ev64)
+    t = v(lambda: V.tensor_scalar(T.e1[:, :], T.evs[:, 0:64], T.acol[:, 0:1], None, A.add), a_ev)
+    t = v(lambda: V.tensor_tensor(T.e2[:, :], T.e1[:, :], T.m64[:, :], A.mult), t)
+    t = v(lambda: V.tensor_scalar(T.e3[:, :], T.e2[:, :], T.acol[:, 0:1], None, A.subtract), t)
+    w("y", Y, t)
+    Y.dma_start(T.ev[:, :], T.e3[0:128:64, 0:64]).then_inc(sem.dout, 16)
+    outs += 16
+
+    w("g", g, ("sv", cnt["v"]), ("ss", cnt["s"]), ("st", cnt["t"]), ("sg", cnt["g"]), ("dout", outs), ("loc", loc))

@@ -1,50 +1,46 @@
 from concourse.bass import DstId, RemoteDMATransfer
-from concourse.mybir import dt, AluOpType as A, AxisListType, ActivationFunctionType as F
+from concourse.mybir import dt, AluOpType as A, AxisListType as AX, ActivationFunctionType as F
 
 CODES, PLANE = "float8_e4m3fn_x4", "uint8"
-BIG = 1.0e29
+
+
+def _f32(n):
+    return ("sbuf", [128, n], "float32")
+
+
+_I1 = ("sbuf", [128, 1], "int32")
 SCRATCH = {
-    "snr": ("sbuf", [128, 8], "int32"),
-    "xt": ("sbuf", [128, 520], "bfloat16"),
-    "ut": ("sbuf", [128, 512], "bfloat16"),
-    "wt": ("sbuf", [128, 512], "bfloat16"),
+    "snd": ("dram", [128, 1], "int32"), "snr": ("sbuf", [128, 8], "int32"), "xt": ("sbuf", [128, 520], "bfloat16"),
+    "ut": ("sbuf", [128, 512], "bfloat16"), "wt": ("sbuf", [128, 512], "bfloat16"),
     "xq": ("sbuf", [128, 130], CODES), "xs": ("sbuf", [128, 130], PLANE),
     "uq": ("sbuf", [128, 128], CODES), "us": ("sbuf", [128, 128], PLANE),
     "ur": ("sbuf", [128, 128], CODES), "urs": ("sbuf", [128, 128], PLANE),
     "wq": ("sbuf", [128, 128], CODES), "ws": ("sbuf", [128, 128], PLANE),
     "kq": ("sbuf", [128, 576], CODES), "kp": ("sbuf", [128, 576], PLANE),
     "pq": ("sbuf", [128, 128], CODES), "ps": ("sbuf", [128, 128], PLANE),
-    "fwl": ("sbuf", [128, 2], "uint16"),
-    "fwq": ("sbuf", [128, 32], CODES), "fws": ("sbuf", [128, 32], PLANE),
-    "rl": ("sbuf", [128, 8], "uint16"),
+    "fwl": ("dram", [128, 1], "int32"), "fwq": ("sbuf", [128, 32], CODES), "fws": ("sbuf", [128, 32], PLANE),
+    "land": ("dram", [8, 128, 1], "int32"), "row": ("sbuf", [128, 1024], "int32"),
     "lq": ("sbuf", [128, 128], CODES), "ls": ("sbuf", [128, 128], PLANE),
-    "oq": ("sbuf", [128, 512], CODES), "os_": ("sbuf", [128, 512], PLANE),
+    "oq": ("sbuf", [128, 512], CODES), "op": ("sbuf", [128, 512], PLANE),
     "lst": ("sbuf", [128, 8], "uint16"), "lo": ("sbuf", [128, 2], "uint16"),
     "zo": ("sbuf", [128, 8], "uint16"), "coff": ("sbuf", [128, 4], "uint16"),
-    "loff": ("sbuf", [128, 32], "uint16"), "roff": ("sbuf", [128, 32], "uint16"),
-    "pi": ("sbuf", [128, 1], "int32"), "pm": ("sbuf", [128, 1], "int32"), "pmf": ("sbuf", [128, 1], "float32"),
-    "q16": ("sbuf", [128, 32], "float32"), "jw": ("sbuf", [128, 32], "float32"), "jm": ("sbuf", [128, 32], "float32"),
-    "kb": ("sbuf", [128, 4], "float32"), "ft": ("sbuf", [128, 136], "float32"), "zr": ("sbuf", [128, 128], "float32"),
-    "neg": ("sbuf", [128, 512], "float32"), "mk": ("sbuf", [128, 512], "float32"),
-    "k64": ("sbuf", [128, 64], "float32"), "acol": ("sbuf", [128, 4], "float32"),
-    "sm": ("sbuf", [128, 512], "float32"),
+    "loff": ("sbuf", [128, 32], "uint16"), "roff": ("sbuf", [128, 16], "uint16"),
+    "qall": ("sbuf", [128, 2], "uint16"), "qown": ("sbuf", [128, 2], "uint16"),
+    "pi": _I1, "pm": _I1, "pm32": _I1, "ia": _I1, "ib": _I1, "ic": _I1, "id5": _I1,
+    "pmf": _f32(1), "fa": _f32(1), "fx": _f32(1), "fc": _f32(1), "fd": _f32(1), "is0": _f32(1), "nm": _f32(1),
+    "q16": _f32(32), "jw": _f32(32), "kb": _f32(4), "zr": _f32(128), "k64": _f32(64), "jio": _f32(128), "jrow": _f32(128),
     "c0": ("sbuf", [128, 640], "bfloat16"), "c1": ("sbuf", [128, 640], "bfloat16"),
     "c2": ("sbuf", [128, 640], "bfloat16"), "c3": ("sbuf", [128, 640], "bfloat16"),
-    "junk": ("sbuf", [128, 640], "bfloat16"), "scn": ("sbuf", [128, 320], "float32"),
-    "tin": ("sbuf", [128, 128], "float32"), "tt": ("sbuf", [128, 128], "float32"),
-    "rin": ("sbuf", [128, 32], "float32"), "rwp": ("sbuf", [128, 32], "float32"), "rw": ("sbuf", [128, 32], "float32"),
-    "dd": ("sbuf", [128, 32], "float32"), "lm": ("sbuf", [128, 32], "float32"), "lt": ("sbuf", [128, 32], "float32"),
-    "fl": ("sbuf", [128, 128], "float32"), "pinc": ("sbuf", [128, 128], "float32"), "zq": ("sbuf", [128, 4], "float32"),
-    "m64": ("sbuf", [128, 64], "float32"),
-    "evin": ("sbuf", [128, 512], "float32"), "evs": ("sbuf", [128, 512], "float32"),
-    "e1": ("sbuf", [128, 64], "float32"), "e2": ("sbuf", [128, 64], "float32"), "e3": ("sbuf", [128, 64], "float32"),
-    "yb": ("sbuf", [128, 512], "float32"),
+    "junk": ("sbuf", [128, 640], "bfloat16"), "junv": ("sbuf", [128, 128], "bfloat16"),
+    "tb": _f32(448), "tt": _f32(128), "rin": _f32(32), "rwp": _f32(32), "l1": _f32(32), "l2": _f32(32), "l3": _f32(32),
+    "fl": _f32(128), "pin1": _f32(128), "pinc": _f32(128), "zq": _f32(4), "zv": _f32(4), "m64": _f32(64),
+    "evi": _f32(128), "ev2": _f32(128), "evw": _f32(512), "ep": _f32(256), "e1": _f32(128), "e2": _f32(64), "e3": _f32(64),
+    "e4": _f32(64), "yb": _f32(512),
     "pr": ("psum", [128, 512], "float32"), "pc": ("psum", [128, 2048], "float32"),
     "p2": ("psum", [128, 512], "float32"), "py": ("psum", [128, 1024], "float32"),
 }
-SEMAPHORES = ["sv", "ss", "st", "sg", "dsn", "dx", "du", "dk", "dw", "down", "dr", "dout",
-              "aL", "aC", "aS", "fL", "fC", "fS", "loc"]
-KINDS = ("L", "C", "S")
+SEMAPHORES = ["sv", "ss", "st", "sg", "dsn", "dsd", "dx", "du", "dk", "dw", "down", "drow", "dr", "dev", "dout",
+              "aL", "aC", "aS", "fC", "fS", "loc"]
 
 
 def bits(es):
@@ -52,38 +48,6 @@ def bits(es):
     for e in es:
         m |= 1 << e
     return m
-
-
-def plan(s, T, topo):
-    core = T.cores[s]
-    n = len(T.cores)
-    cross = [d for d in range(n) if d != s and not topo.may_write(core, T.cores[d])]
-    home = [d for d in range(n) if d not in cross]
-    same = [d for d in home if d != s]
-    ports = [f for f in topo.cores_of(core) if f != core and all(topo.may_write(f, T.cores[d]) for d in cross)]
-    near = [f for f in ports if topo.die(f) == topo.die(core)][0]
-    far = [f for f in ports if topo.die(f) != topo.die(core)][0]
-    fw = [near, far] if (s // 2) % 2 == 0 else [far, near]
-    off = topo.engines(core, T.cores[same[0]])
-    on = [e for e in topo.engines(core, near) if e not in off]
-    h = len(on) // 2
-    hop = [(fw[0], on[:h], cross[:2]), (fw[1], on[h:], cross[2:])]
-    q = len(off) // 4
-    parts = {"L": (off[:2 * q], off[2 * q:3 * q], off[3 * q:]),
-             "C": (off[:2 * q], off[2 * q:3 * q], off[3 * q:]),
-             "S": (off[2 * q:], off[:q], off[q:2 * q])}
-    return {"core": core, "cross": cross, "home": home, "same": same, "hop": hop, "parts": parts}
-
-
-def onward(f, dst, i, topo):
-    es = topo.engines(f, dst)
-    h = len(es) // 2
-    return es[:h] if i == 0 else es[h:]
-
-
-def xfer(src_core, dst_core, es, sem, src, dst, topo):
-    rid, pid = topo.addr(dst_core, src_core)
-    return RemoteDMATransfer(dst_ids=[DstId(rid=rid, pnc=pid)], dma_engine_mask=bits(es), remote_sem=sem, srcs=[src], dsts=[dst])
 
 
 def u8(v):
@@ -94,107 +58,150 @@ def u32(v):
     return v.bitcast(dt.uint32)
 
 
+def split(es, n, turn=0):
+    if n == 1:
+        return [es]
+    h = len(es) // 2
+    if n == 2:
+        return [es[:h], es[h:]]
+    q = h // 2
+    wide, rest = (es[:h], [es[h:h + q], es[h + q:]]) if turn % 2 == 0 else (es[h:], [es[:q], es[q:h]])
+    return rest[:turn] + [wide] + rest[turn:]
+
+
+def plan(s, T, topo):
+    core = T.cores[s]
+    n = len(T.cores)
+    cross = [d for d in range(n) if d != s and not topo.may_write(core, T.cores[d])]
+    home = [d for d in range(n) if d not in cross]
+    same = [d for d in home if d != s]
+    chip = [f for f in topo.cores_of(core) if f != core]
+    ports = [f for f in chip if all(topo.may_write(f, T.cores[d]) for d in cross)]
+    near = [f for f in ports if topo.die(f) == topo.die(core)]
+    far = [f for f in ports if topo.die(f) != topo.die(core)]
+    a, b = (near, far) if (s // 2) % 2 == 0 else (far, near)
+    off = topo.engines(core, T.cores[same[0]])
+    on = [e for e in topo.engines(core, near[0]) if e not in off]
+    h = len(on) // 2
+    hop = [(k, es, f, ds) for i, k in enumerate("CS") for es, f, ds in ((on[:h], a[i], cross[:2]), (on[h:], b[i], cross[2:]))]
+    straight = [(k, es, d) for i, k in enumerate("CS") for es, d in zip(split(off, 3, i), same)]
+    return {"core": core, "cross": cross, "home": home, "same": same, "order": cross + home, "on": on, "off": off,
+            "list": list(zip([a[0], a[1], b[0], b[1]], cross)), "hop": hop, "straight": straight}
+
+
+def last_leg(f, ds, T, topo):
+    return split(topo.engines(f, T.cores[ds[0]]), len(ds))
+
+
+def xfer(src_core, dst_cores, es, sem, src, dsts, topo):
+    ids = []
+    for d in dst_cores:
+        rid, pid = topo.addr(d, src_core)
+        ids.append(DstId(rid=rid, pnc=pid))
+    return RemoteDMATransfer(dst_ids=ids, dma_engine_mask=bits(es), remote_sem=sem, srcs=[src], dsts=dsts)
+
+
+def part(T, k, codes, plane, i, n):
+    return u8(T[codes][:, 16 * i:16 * (i + n)]) if k == "C" else T[plane][:, 16 * i:16 * (i + n)]
+
+
 def forward(g, core, s, T, topo):
     p = plan(s, T, topo)
     loc = 0
-    for f, es, ds in p["hop"]:
-        if f != core:
-            continue
-        for k in KINDS:
+    for f, d in p["list"]:
+        if f == core:
+            es = topo.engines(core, T.cores[d])[:1]
+            g.wait_ge(T.sem.aL, 1)
+            g.remote_dma_fused([xfer(core, [T.cores[d]], es, T.sem.aL, T.fwl[:, :], [T.land[s]], topo)], local_sem=T.sem.loc)
+            loc += len(es)
+    for k, es, f, ds in p["hop"]:
+        if f == core:
             g.wait_ge(T.sem["f" + k], len(es))
             ts = []
-            for i, d in enumerate(ds):
-                dc = T.cores[d]
-                me = onward(core, dc, i, topo)
-                if k == "L":
-                    a, b = T.fwl[:, i:i + 1], T.rl[:, s:s + 1]
-                elif k == "C":
-                    a, b = u8(T.fwq[:, 16 * i:16 * i + 16]), u8(T.lq[:, 16 * s:16 * s + 16])
-                else:
-                    a, b = T.fws[:, 16 * i:16 * i + 16], T.ls[:, 16 * s:16 * s + 16]
-                ts.append(xfer(core, dc, me, T.sem["a" + k], a, b, topo))
+            for i, (d, me) in enumerate(zip(ds, last_leg(core, ds, T, topo))):
+                ts.append(xfer(core, [T.cores[d]], me, T.sem["a" + k], part(T, k, "fwq", "fws", i, 1),
+                               [part(T, k, "lq", "ls", s, 1)], topo))
                 loc += len(me)
             g.remote_dma_fused(ts, local_sem=T.sem.loc)
+    if loc:
         g.wait_ge(T.sem.loc, loc)
 
 
 def rank_program(g, core, T, topo):
     r = T.rank_of(core)
+    n = len(T.cores)
     if r is None:
-        for s in range(len(T.cores)):
+        for s in range(n):
             if T.cores[s] in topo.cores_of(core):
                 forward(g, core, s, T, topo)
         return
-    n = len(T.cores)
     P = plan(r, T, topo)
     V, S, E, Y = g.vector, g.scalar, g.tensor, g.sync
     sem = T.sem
+    queue = {"v": V, "s": S, "t": E, "g": g, "y": Y}
     cnt = {"v": 0, "s": 0, "t": 0, "g": 0}
     seen = {}
 
-    def done(q, inst):
-        inst.then_inc(sem["s" + q], 1)
-        cnt[q] += 1
-        return ("s" + q, cnt[q])
+    def w(name, *tags):
+        for sn, val in tags:
+            if seen.get((name, sn), 0) < val:
+                queue[name].wait_ge(sem[sn], val)
+                seen[(name, sn)] = val
 
-    def w(name, queue, *tags):
-        for sn, v in tags:
-            if seen.get((name, sn), 0) < v:
-                queue.wait_ge(sem[sn], v)
-                seen[(name, sn)] = v
+    def do(name, call, tags):
+        w(name, *tags)
+        call().then_inc(sem["s" + name], 1)
+        cnt[name] += 1
+        return ("s" + name, cnt[name])
 
     def v(call, *tags):
-        w("v", V, *tags)
-        return done("v", call())
+        return do("v", call, tags)
 
     def sc(call, *tags):
-        w("s", S, *tags)
-        return done("s", call())
+        return do("s", call, tags)
 
     def mm(call, *tags):
-        w("t", E, *tags)
-        return done("t", call())
+        return do("t", call, tags)
 
     def gg(call, *tags):
-        w("g", g, *tags)
-        return done("g", call())
+        return do("g", call, tags)
 
-    need = {"L": 0, "C": 0, "S": 0}
+    need = {"L": n - 1, "C": 0, "S": 0}
     for s in range(n):
         if s == r:
             continue
         p = plan(s, T, topo)
-        for k in KINDS:
-            for f, es, ds in p["hop"]:
-                if r in ds:
-                    need[k] += len(onward(f, core, ds.index(r), topo))
-            if r in p["same"]:
-                need[k] += len(p["parts"][k][p["same"].index(r)])
+        for k, es, f, ds in p["hop"]:
+            if r in ds:
+                need[k] += len(last_leg(f, ds, T, topo)[ds.index(r)])
+        for k, es, d in p["straight"]:
+            if d == r:
+                need[k] += len(es)
 
-    for k in range(4):
-        Y.dma_start(T.snr[16 * k:16 * k + 16, :], T.sn[:, :]).then_inc(sem.dsn, 16)
-        S.dma_start(T.snr[64 + 16 * k:80 + 16 * k, :], T.sn[:, :]).then_inc(sem.dsn, 16)
-    Y.dma_start(T.xt[:, 8:520], T.x[:, :]).then_inc(sem.dx, 16)
-    S.dma_start(T.ut[:, 0:8], T.u[:, 0:8]).then_inc(sem.du, 16)
-    S.dma_start(u8(T.kq[:, 0:512]), T.kc[:, :]).then_inc(sem.dk, 16)
-    Y.dma_start(T.kp[:, 0:512], T.ks[:, :]).then_inc(sem.dk, 16)
+    Y.dma_start(T.snd[:, :], T.sn[:, :]).then_inc(sem.dsd, 16)
+    S.dma_start(T.xt[:, 8:520], T.x[:, :]).then_inc(sem.dx, 16)
+    for k in range(8):
+        (Y if k < 4 else S).dma_start(T.snr[16 * k:16 * k + 16, :], T.sn[:, :]).then_inc(sem.dsn, 16)
+    Y.dma_start(T.ut[:, 0:8], T.u[:, 0:8]).then_inc(sem.du, 16)
+    S.dma_start(T.kp[:, 64:576], T.ks[:, :]).then_inc(sem.dk, 16)
+    Y.dma_start(u8(T.kq[:, 64:576]), T.kc[:, :]).then_inc(sem.dk, 16)
     Y.dma_start(T.wt[:, :], T.w[:, :]).then_inc(sem.dw, 16)
+    Y.dma_start(T.land[r], T.sn[:, :]).then_inc(sem.down, 16)
     SN, DX, DU, DK, DW = ("dsn", 128), ("dx", 16), ("du", 16), ("dk", 32), ("dw", 16)
 
-    a_neg = v(lambda: V.memset(T.neg[:, :], -BIG))
     a_x0 = v(lambda: V.memset(T.xt[:, 0:8], 0.0))
     a_u0 = v(lambda: V.memset(T.ut[:, 8:512], 0.0))
     a_zo = v(lambda: V.memset(T.zo[:, :], 0))
     a_pi = gg(lambda: g.iota(T.pi[:, :], [[1, 1]], 0, 1))
     a_q16 = gg(lambda: g.iota(T.q16[:, :], [[16, 32]], 0, 0, allow_small_or_imprecise_dtypes=True))
-    a_mk = gg(lambda: g.affine_select(T.mk[:, :], T.neg[:, :], [[0, 4], [-1, 128]], A.is_gt, BIG, 0, 1), a_neg)
-    a_ft = v(lambda: V.memset(T.ft[:, 2:136], 1.0))
-    a_ft = v(lambda: V.memset(T.ft[:, 0:2], 0.0))
-    v(lambda: V.memset(T.zr[:, :], 0.0))
-    v(lambda: V.memset(T.tin[:, :], 0.0))
-    v(lambda: V.memset(T.evin[32:64, :], 0.0))
-    t = v(lambda: V.memset(T.acol[:, :], 0.0))
-    a_con = v(lambda: V.memset(T.acol[0:32, :], 1.0), t)
+    a_jio = gg(lambda: g.iota(T.jio[:, :], [[1, 128]], 1, 4, allow_small_or_imprecise_dtypes=True))
+    t1 = v(lambda: V.tensor_scalar(T.ia[:, :], T.pi[:, :], 1, 3, A.logical_shift_right, A.bitwise_and), a_pi)
+    t2 = v(lambda: V.tensor_scalar(T.ib[:, :], T.pi[:, :], 1, None, A.bitwise_and))
+    t3 = v(lambda: V.tensor_scalar(T.ic[:, :], T.pi[:, :], 3, 1, A.logical_shift_right, A.bitwise_and))
+    t4 = v(lambda: V.tensor_scalar(T.id5[:, :], T.pi[:, :], 5, None, A.logical_shift_right))
+    t1 = v(lambda: V.tensor_scalar(T.fa[:, :], T.ia[:, :], 8, None, A.mult), t1)
+    t3 = v(lambda: V.tensor_scalar(T.fc[:, :], T.ic[:, :], 2, None, A.mult), t3)
+    t5 = v(lambda: V.tensor_scalar(T.pm32[:, :], T.pi[:, :], 31, None, A.bitwise_and))
 
     cx, hm = P["cross"], P["home"]
     stx, sth = cx[1] - cx[0], hm[1] - hm[0]
@@ -203,161 +210,157 @@ def rank_program(g, core, T, topo):
     a_lo = v(lambda: V.tensor_scalar(T.lo[:, 0:1], T.snr[:, r:r + 1], 2, None, A.add))
     a_xq = v(lambda: V.quantize_mx(T.xq[:, 0:130], T.xs[:, 0:130], T.xt[:, 0:520]), DX, a_x0)
 
-    def pick(o, os_, i, is_, b, off, lo, vt, st):
-        a, e = o
-        c, d = i
-        x = v(lambda: V.tensor_copy(u32(T[a][:, e[0]:e[1]]), u32(T[c][:, d[0]:d[1]]).indirect(T[off][:, lo[0]:lo[1]])), *vt)
-        y = sc(lambda: S.activation(T[os_][:, e[0]:e[1]], T[is_][:, d[0]:d[1]].indirect(T[off][:, lo[0]:lo[1]]), F.Copy), *st)
+    def pick(o, oc, i, ic, off, lc, vt, st):
+        x = v(lambda: V.tensor_copy(u32(T[o[0]][:, oc[0]:oc[1]]), u32(T[i[0]][:, ic[0]:ic[1]]).indirect(T[off][:, lc[0]:lc[1]])), *vt)
+        y = sc(lambda: S.activation(T[o[1]][:, oc[0]:oc[1]], T[i[1]][:, ic[0]:ic[1]].indirect(T[off][:, lc[0]:lc[1]]), F.Copy), *st)
         return x, y
 
-    X = ("xq", (0, 130))
-    pxc, pxs = pick(("pq", (0, 64)), "ps", X, "xs", None, "lst", (0, 4), (a_xq, a_lx), (a_xq, a_lx))
-    pyc, pys = pick(("pq", (64, 128)), "ps", X, "xs", None, "lst", (4, 8), (a_ly,), (a_ly,))
-    poc, pos = pick(("lq", (16 * r, 16 * r + 16)), "ls", X, "xs", None, "lo", (0, 1), (a_lo,), (a_lo,))
-    w("y", Y, a_lo)
-    Y.dma_start(T.rl[:, r:r + 1], T.lo[:, 0:1]).then_inc(sem.down, 16)
+    X, XW = ("xq", "xs"), (0, 130)
+    px = pick(("pq", "ps"), (0, 64), X, XW, "lst", (0, 4), (a_xq, a_lx), (a_xq, a_lx))
+    py = pick(("pq", "ps"), (64, 128), X, XW, "lst", (4, 8), (a_ly,), (a_ly,))
 
     loc = 0
 
-    def hop1(k):
-        tot = 0
-        ts = []
-        for i, (f, es, ds) in enumerate(P["hop"]):
-            if k == "L":
-                a, b = T.lst[:, 2 * i:2 * i + 2], T.fwl[:, 0:2]
-            elif k == "C":
-                a, b = u8(T.pq[:, 32 * i:32 * i + 32]), u8(T.fwq[:, 0:32])
-            else:
-                a, b = T.ps[:, 32 * i:32 * i + 32], T.fws[:, 0:32]
-            ts.append(xfer(core, f, es, sem["f" + k], a, b, topo))
-            tot += len(es)
+    def send(ts, es):
         g.remote_dma_fused(ts, local_sem=sem.loc)
-        return tot
+        return sum(len(e) for e in es)
+
+    def hop(k):
+        calls = [c for c in P["hop"] if c[0] == k]
+        return send([xfer(core, [f], es, sem["f" + k], part(T, k, "pq", "ps", P["order"].index(ds[0]), 2),
+                          [part(T, k, "fwq", "fws", 0, 2)], topo) for _, es, f, ds in calls], [c[1] for c in calls])
 
     def straight(k):
-        tot = 0
-        ts = []
-        for i, d in enumerate(P["same"]):
-            es = P["parts"][k][i]
-            j = 4 + hm.index(d)
-            if k == "L":
-                a, b = T.lst[:, j:j + 1], T.rl[:, r:r + 1]
-            elif k == "C":
-                a, b = u8(T.pq[:, 16 * j:16 * j + 16]), u8(T.lq[:, 16 * r:16 * r + 16])
-            else:
-                a, b = T.ps[:, 16 * j:16 * j + 16], T.ls[:, 16 * r:16 * r + 16]
-            ts.append(xfer(core, T.cores[d], es, sem["a" + k], a, b, topo))
-            tot += len(es)
-        g.remote_dma_fused(ts, local_sem=sem.loc)
-        return tot
+        calls = [c for c in P["straight"] if c[0] == k]
+        return send([xfer(core, [T.cores[d]], es, sem["a" + k], part(T, k, "pq", "ps", P["order"].index(d), 1),
+                          [part(T, k, "lq", "ls", r, 1)], topo) for _, es, d in calls], [c[1] for c in calls])
 
-    w("g", g, a_lx)
-    loc += hop1("L")
-    w("g", g, pxc)
-    loc += hop1("C")
-    w("g", g, pxs)
-    loc += hop1("S")
-    w("g", g, a_ly)
-    loc += straight("L")
-    w("g", g, pyc)
+    w("g", ("dsd", 16))
+    fs = [f for f, d in P["list"]]
+    le = [P["on"][:1], P["off"][:1]]
+    loc += send([xfer(core, fs, le[0], sem.aL, T.snd[:, :], [T.fwl[:, :] for f in fs], topo),
+                 xfer(core, [T.cores[d] for d in P["same"]], le[1], sem.aL, T.snd[:, :], [T.land[r] for d in P["same"]], topo)], le)
+    w("g", px[0])
+    loc += hop("C")
+    w("g", px[1])
+    loc += hop("S")
+    w("g", py[0])
     loc += straight("C")
-    w("g", g, pys)
+    w("g", py[1])
     loc += straight("S")
-    a_jr = gg(lambda: g.iota(T.evin[0:32, :], [[1, 512]], 0, 0, allow_small_or_imprecise_dtypes=True))
-    a_k64 = gg(lambda: g.iota(T.k64[:, :], [[1, 64]], 0, 0, allow_small_or_imprecise_dtypes=True))
 
     a_uq = v(lambda: V.quantize_mx(T.uq[:, :], T.us[:, :], T.ut[:, :]), DU, a_u0)
-    urc, urs = pick(("ur", (0, 128)), "urs", ("uq", (0, 128)), "us", None, "zo", (0, 8), (a_uq, a_zo), (a_uq, a_zo))
-    a_row = mm(lambda: E.matmul_mx(T.pr[:, :], T.ur[:, :], T.urs[:, :], T.kq[:, 0:512], T.kp[:, 0:512], True, True), DK, urc, urs)
-    a_col = []
-    for c in range(4):
-        a_col.append(mm(lambda: E.matmul_mx(T.pc[:, 512 * c:512 * c + 128], T.kq[:, 128 * c:128 * c + 128],
-                                            T.kp[:, 128 * c:128 * c + 128], T.ur[:, :], T.urs[:, :], True, True)))
-    a_row2 = mm(lambda: E.matmul_mx(T.p2[:, :], T.ur[:, :], T.urs[:, :], T.kq[:, 0:512], T.kp[:, 0:512], True, True))
-    t = v(lambda: V.tensor_scalar(T.pm[:, :], T.pi[:, :], 15, None, A.bitwise_and), a_pi)
+    ur = pick(("ur", "urs"), (0, 128), ("uq", "us"), (0, 128), "zo", (0, 8), (a_uq, a_zo), (a_uq, a_zo))
+    po = pick(("lq", "ls"), (16 * r, 16 * r + 16), X, XW, "lo", (0, 1), (a_lo,), (a_lo,))
+    a_row = mm(lambda: E.matmul_mx(T.pr[:, :], T.ur[:, :], T.urs[:, :], T.kq[:, 64:576], T.kp[:, 64:576], True, True), DK, *ur)
+    turn = (1, 2, 3, 0)
+    a_col = {}
+    for c in turn:
+        lo, hi = 64 + 128 * c, 192 + 128 * c
+        a_col[c] = mm(lambda: E.matmul_mx(T.pc[:, 512 * c:512 * c + 128], T.kq[:, lo:hi], T.kp[:, lo:hi],
+                                          T.ur[:, :], T.urs[:, :], True, True))
+    a_row2 = mm(lambda: E.matmul_mx(T.p2[:, :], T.ur[:, :], T.urs[:, :], T.kq[:, 64:576], T.kp[:, 64:576], True, True))
+    a_tin = v(lambda: V.memset(T.tb[:, 320:448], 0.0))
+    t1 = v(lambda: V.tensor_tensor(T.fx[:, :], T.fa[:, :], T.ib[:, :], A.add), t1, t2)
+    t = v(lambda: V.tensor_scalar(T.pm[:, :], T.pi[:, :], 15, None, A.bitwise_and))
+    t4 = v(lambda: V.tensor_scalar(T.fd[:, :], T.id5[:, :], 2, None, A.mult), t4)
+    a_pm = v(lambda: V.tensor_scalar(T.qall[:, 0:1], T.fx[:, :], T.fc[:, 0:1], None, A.add), t1, t3)
+    a_pm = v(lambda: V.tensor_scalar(T.qall[:, 1:2], T.fx[:, :], T.fc[:, 0:1], 4.0, A.add, A.add))
     t = v(lambda: V.tensor_copy(T.pmf[:, :], T.pm[:, :]), t)
-    a_jw = v(lambda: V.tensor_scalar(T.jw[:, :], T.q16[:, :], T.pmf[:, 0:1], None, A.add), t, a_q16)
-    a_jm = v(lambda: V.tensor_scalar(T.jm[:, :], T.q16[:, :], T.pmf[:, 0:1], -512.0, A.add, A.add))
-    a_kb = v(lambda: V.tensor_scalar(T.kb[:, :], T.q16[:, 0:4], T.pmf[:, 0:1], 0.5, A.add, A.add))
-    a_wq = v(lambda: V.quantize_mx(T.wq[:, :], T.ws[:, :], T.wt[:, :]), DW)
+    a_pq = v(lambda: V.tensor_scalar(T.qown[:, 0:1], T.fx[:, :], T.fd[:, 0:1], None, A.add), t4)
+    a_nm = v(lambda: V.tensor_scalar(T.nm[:, :], T.pm32[:, :], 0, None, A.is_gt), t5)
+    a_is0 = v(lambda: V.tensor_scalar(T.is0[:, :], T.pm32[:, :], 0, None, A.is_equal))
 
-    a_sm = v(lambda: V.tensor_tensor(T.sm[:, :], T.pr[:, :], T.mk[:, :], A.max), a_row, a_mk)
     sums = []
-    for c in range(4):
+    for c in turn:
         b = T["c%d" % c]
         sj = T.pc[:, 512 * c:512 * c + 1]
+        own = T.pr[:, 128 * c:128 * c + 128]
+        t0 = v(lambda: V.tensor_scalar(b[:, 512:640], own, sj, None, A.is_equal), a_row, a_col[c])
+        masked = gg(lambda: g.affine_select(b[:, 512:640], b[:, 512:640], [[-1, 128]], A.is_gt, 0.0, 0, 1), t0)
         if c:
-            v(lambda: V.tensor_scalar(b[:, 0:128 * c], T.pr[:, 0:128 * c], sj, None, A.is_le), a_col[c])
-        v(lambda: V.tensor_scalar(b[:, 128 * c:512], T.pr[:, 128 * c:512], sj, None, A.is_lt), a_col[c])
-        t = v(lambda: V.tensor_scalar(b[:, 512:640], T.sm[:, 128 * c:128 * c + 128], sj, None, A.is_equal), a_sm)
-        if c < 3:
-            sums.append(sc(lambda: S.activation(T.junk[:, :], b[:, :], F.Copy, accum_out=T.tin[:, 32 * c:32 * c + 1]), t, a_con,
-                           *sums[-1:]))
+            v(lambda: V.tensor_scalar(b[:, 0:128 * c], T.pr[:, 0:128 * c], sj, None, A.is_le))
+        t0 = v(lambda: V.tensor_scalar(b[:, 128 * c:512], T.pr[:, 128 * c:512], sj, None, A.is_lt))
+        if c:
+            sums.append(sc(lambda: S.activation(T.junk[:, :], b[:, :], F.Copy, accum_out=T.tb[:, 320 + 32 * c:321 + 32 * c]),
+                           t0, masked, a_tin, *sums[-1:]))
         else:
-            t = v(lambda: V.tensor_tensor_scan(T.scn[:, :], b[:, 0:320], b[:, 320:640], 0.0, A.add, A.add), t)
-            sums.append(v(lambda: V.tensor_copy(T.tin[:, 32 * c:32 * c + 1], T.scn[:, 319:320]), t))
-    a_ev64 = sc(lambda: S.activation(T.evin[64:128, :], T.p2[64:128, :], F.Copy), a_row2)
-    a_tt = v(lambda: V.transpose(T.tt[:, :], T.tin[:, :]), *sums)
+            sums.append(v(lambda: V.tensor_tensor_scan(T.tb[:, 1:321], b[:, 0:320], b[:, 320:640], 0.0, A.add, A.add),
+                          t0, masked, a_tin))
+    a_k64 = gg(lambda: g.iota(T.k64[:, :], [[1, 64]], 0, 0, allow_small_or_imprecise_dtypes=True))
+    w("y", ("aL", need["L"]), ("down", 16))
+    Y.dma_start(T.row[0:1, :], T.land[:, :, :]).then_inc(sem.drow, 16)
+    a_tt = v(lambda: V.transpose(T.tt[:, :], T.tb[:, 320:448]), *sums)
     for a in range(4):
-        q, nm = (Y, "y") if a % 2 == 0 else (S, "s")
-        w(nm, q, a_tt)
-        q.dma_start(T.rin[32 * a:32 * a + 32, 0:16], T.tt[0:128:32, 0:128]).then_inc(sem.dr, 16)
+        nm = "sy"[a % 2]
+        w(nm, a_tt)
+        queue[nm].dma_start(T.rin[32 * a:32 * a + 32, 0:16], T.tt[0:128:32, :]).then_inc(sem.dr, 16)
+    a_kb = v(lambda: V.tensor_scalar(T.kb[:, :], T.q16[:, 0:4], T.pmf[:, 0:1], 0.5, A.add, A.add), t, a_q16)
+    a_jw = v(lambda: V.tensor_scalar(T.jw[:, :], T.q16[:, :], T.pmf[:, 0:1], 64.0, A.add, A.add))
+    a_zr = v(lambda: V.memset(T.zr[0:1, :], 0.0))
+    for a in range(4):
+        a_evi = sc(lambda: S.activation(T.evi[32 * a:32 * a + 32, :], T.p2[32 * a:32 * a + 32, 128 * a:128 * a + 128], F.Identity,
+                                        scale=T.nm[32 * a:32 * a + 32, 0:1]), a_row2, a_nm)
+    a_wq = v(lambda: V.quantize_mx(T.wq[:, :], T.ws[:, :], T.wt[:, :]), DW)
 
-    a_fl = v(lambda: V.tensor_copy(T.fl[:, :], T.ft[:, 0:136].indirect(T.rl[:, 0:8])), ("aL", need["L"]), ("down", 16), a_ft)
-    a_pinc = v(lambda: V.tensor_tensor_scan(T.pinc[:, :], T.fl[:, :], T.zr[:, :], 0.0, A.add, A.add), a_fl)
+    t = v(lambda: V.tensor_scalar(T.fl[0:1, :], T.row[0:1, r:1024:8], 0, None, A.is_ge), ("drow", 16))
+    t = v(lambda: V.tensor_tensor_scan(T.pin1[0:1, :], T.fl[0:1, :], T.zr[0:1, :], 0.0, A.add, A.add), t, a_zr)
+    a_pinc = gg(lambda: g.partition_broadcast(T.pinc[:, :], T.pin1[0:1, :], 128), t)
     m = T.pinc[:, 127:128]
-    for q in range(4):
+    a_z = sums[2]
+    for q in range(3):
         a_z = sc(lambda: S.activation(T.junk[:, 0:127], T.pinc[:, 0:127], F.Sign, bias=T.kb[:, q:q + 1], scale=-1.0,
-                                      accum_out=T.zq[:, q:q + 1]), a_pinc, a_kb, sums[2] if q == 0 else a_z)
-    a_m64 = v(lambda: V.tensor_scalar(T.m64[:, :], T.k64[:, :], m, None, A.is_lt), a_pinc, a_k64)
+                                      accum_out=T.zq[:, q:q + 1]), a_pinc, a_kb, a_z)
+    a_jr = v(lambda: V.tensor_scalar(T.jrow[:, :], T.jio[:, :], T.is0[:, 0:1], None, A.mult), a_jio, a_is0)
+    a_w0 = v(lambda: V.memset(T.evw[:, 0:64], 0.0))
+    a_ev2 = v(lambda: V.tensor_tensor(T.ev2[:, :], T.evi[:, :], T.jrow[:, :], A.add), a_evi, a_jr)
+    t1 = v(lambda: V.tensor_scalar(T.junv[:, 0:127], T.pinc[:, 0:127], T.kb[:, 3:4], None, A.is_le), a_pinc)
+    a_m64 = v(lambda: V.tensor_scalar(T.m64[0:2, :], T.k64[0:2, :], T.pinc[0:2, 127:128], None, A.is_lt), a_k64)
+    t1 = v(lambda: V.tensor_reduce(T.zv[:, 0:1], T.junv[:, 0:127], AX.X, A.add), t1)
     t = v(lambda: V.tensor_copy(T.rin[:, 16:32], T.rin[:, 0:16]), ("dr", 64))
+    a_c3 = v(lambda: V.tensor_copy(T.coff[:, 3:4], T.zv[:, 0:1]), t1)
     a_rwp = v(lambda: V.transpose(T.rwp[:, :], T.rin[:, :]), t)
-    for a in range(4):
-        for h in range(2):
-            a_rw = v(lambda: V.tensor_copy(T.rw[:, 2 * a + h:32:8], T.rwp[:, 8 * a + h:8 * a + 8:2]), a_rwp)
-    a_dd = v(lambda: V.tensor_tensor(T.dd[:, :], T.rw[:, :], T.jm[:, :], A.subtract), a_rw, a_jm)
-    a_lm = v(lambda: V.tensor_scalar(T.lm[:, :], T.rw[:, :], m, None, A.is_lt))
-    t = v(lambda: V.tensor_tensor(T.lt[:, :], T.dd[:, :], T.lm[:, :], A.mult), a_dd, a_lm)
-    a_loff = v(lambda: V.tensor_tensor(T.lt2[:, :] if False else T.dd[:, :], T.lt[:, :], T.jw[:, :], A.add), t, a_jw)
-    a_loff = v(lambda: V.tensor_copy(T.loff[:, :], T.dd[:, :]), a_loff)
-    a_roff = v(lambda: V.tensor_copy(T.roff[:, :], T.rw[:, :]), a_rw)
-    a_coff = v(lambda: V.tensor_scalar(T.coff[:, :], T.zq[:, :], 0.5, 63.5, A.mult, A.add), a_z)
+    t = v(lambda: V.tensor_scalar(T.l1[:, :], T.rwp[:, :].indirect(T.qall[:, 0:2]), m, 2048.0, A.is_ge, A.mult), a_rwp, a_pm)
+    a_roff = v(lambda: V.tensor_copy(T.roff[:, :], T.rwp[:, :].indirect(T.qown[:, 0:1])), a_pq)
+    t = v(lambda: V.tensor_tensor(T.l2[:, :], T.rwp[:, :].indirect(T.qall[:, 0:2]), T.l1[:, :], A.max), t)
+    t = v(lambda: V.tensor_tensor(T.l3[:, :], T.l2[:, :], T.jw[:, :], A.min), t, a_jw)
+    a_ev = v(lambda: V.tensor_copy(T.evw[:, 0:512].indirect(T.roff[:, 0:8]), T.ev2[:, :]), a_roff, a_ev2, a_w0)
+    a_loff = v(lambda: V.tensor_copy(T.loff[:, :], T.l3[:, :]), t)
+    a_coff = v(lambda: V.tensor_scalar(T.coff[:, 0:3], T.zq[:, 0:3], 0.5, 63.5, A.mult, A.add), a_z)
+    w("y", a_ev)
+    for i in range(2):
+        Y.dma_start(T.ep[i:i + 1, :], T.evw[i:128:32, 0:64]).then_inc(sem.dev, 16)
 
-    cc, cs = pick(("kq", (512, 576)), "kp", ("lq", (0, 128)), "ls", None, "coff", (0, 4),
-                  (("aC", need["C"]), poc, a_coff), (("aS", need["S"]), pos, a_coff))
+    cc, cs = pick(("kq", "kp"), (0, 64), ("lq", "ls"), (0, 128), "coff", (0, 4),
+                  (("aC", need["C"]), po[0], a_coff, a_c3), (("aS", need["S"]), po[1], a_coff, a_c3))
     fin = []
     for h in range(2):
-        x, y = pick(("oq", (256 * h, 256 * h + 256)), "os_", ("kq", (0, 576)), "kp", None, "loff", (16 * h, 16 * h + 16),
-                    (cc, a_loff), (cs, a_loff))
-        fin.append((x, y))
-    ym = []
+        fin.append(pick(("oq", "op"), (256 * h, 256 * h + 256), ("kq", "kp"), (0, 576), "loff", (16 * h, 16 * h + 16),
+                        (cc, a_loff), (cs, a_loff)))
+    yc = []
     for h in range(2):
         lo, hi = 256 * h, 256 * h + 256
-        ym.append(mm(lambda: E.matmul_mx(T.py[:, 512 * h:512 * h + 256], T.wq[:, :], T.ws[:, :], T.oq[:, lo:hi], T.os_[:, lo:hi],
-                                         True, True), a_wq, *fin[h]))
-    yc = [sc(lambda: S.activation(T.yb[:, 0:256], T.py[:, 0:256], F.Copy), ym[0]),
-          v(lambda: V.tensor_copy(T.yb[:, 256:512], T.py[:, 512:768]), ym[1])]
-    outs = 0
-    for h in range(2):
-        w("y", Y, fin[h][0])
-        Y.dma_start(T.oc[:, 1024 * h:1024 * h + 1024], u8(T.oq[:, 256 * h:256 * h + 256])).then_inc(sem.dout, 16)
-        outs += 16
-    for h in range(2):
-        w("y", Y, yc[h])
-        Y.dma_start(T.y[:, 256 * h:256 * h + 256], T.yb[:, 256 * h:256 * h + 256]).then_inc(sem.dout, 16)
-        outs += 16
-        if h == 0:
-            w("y", Y, fin[1][1])
-            for k in range(4):
-                Y.dma_start(T.osc[4 * k:4 * k + 4, :], T.os_[32 * k:32 * k + 4, :]).then_inc(sem.dout, 16)
-                outs += 16
+        ym = mm(lambda: E.matmul_mx(T.py[:, 512 * h:512 * h + 256], T.wq[:, :], T.ws[:, :], T.oq[:, lo:hi], T.op[:, lo:hi],
+                                    True, True), a_wq, *fin[h])
+        yc.append(v(lambda: V.tensor_copy(T.yb[:, lo:hi], T.py[:, 512 * h:512 * h + 256]), ym))
+    t = v(lambda: V.tensor_tensor(T.e1[0:2, :], T.ep[0:2, 0:128], T.ep[0:2, 128:256], A.add), ("dev", 32))
+    t = v(lambda: V.tensor_tensor(T.e2[0:2, :], T.e1[0:2, 0:64], T.e1[0:2, 64:128], A.add), t)
+    t = v(lambda: V.tensor_tensor(T.e3[0:2, :], T.e2[0:2, :], T.m64[0:2, :], A.mult), t, a_m64)
+    a_e4 = v(lambda: V.tensor_scalar(T.e4[0:2, :], T.e3[0:2, :], T.is0[0:2, 0:1], None, A.subtract), t)
 
-    a_ev = v(lambda: V.tensor_copy(T.evs[:, 0:512].indirect(T.roff[:, 0:32]), T.evin[:, :]), a_roff, a_jr, a_ev64)
-    t = v(lambda: V.tensor_scalar(T.e1[:, :], T.evs[:, 0:64], T.acol[:, 0:1], None, A.add), a_ev)
-    t = v(lambda: V.tensor_tensor(T.e2[:, :], T.e1[:, :], T.m64[:, :], A.mult), t)
-    t = v(lambda: V.tensor_scalar(T.e3[:, :], T.e2[:, :], T.acol[:, 0:1], None, A.subtract), t)
-    w("y", Y, t)
-    Y.dma_start(T.ev[:, :], T.e3[0:128:64, 0:64]).then_inc(sem.dout, 16)
-    outs += 16
+    outs = [0]
 
-    w("g", g, ("sv", cnt["v"]), ("ss", cnt["s"]), ("st", cnt["t"]), ("sg", cnt["g"]), ("dout", outs), ("loc", loc))
+    def store(nm, tag, o, i):
+        w(nm, tag)
+        queue[nm].dma_start(o, i).then_inc(sem.dout, 16)
+        outs[0] += 16
+
+    for h in range(2):
+        store("y", fin[h][0], T.oc[:, 1024 * h:1024 * h + 1024], u8(T.oq[:, 256 * h:256 * h + 256]))
+    for k in range(4):
+        store("s", fin[1][1], T.osc[4 * k:4 * k + 4, :], T.op[32 * k:32 * k + 4, :])
+    for h in range(2):
+        store("y", yc[h], T.y[:, 256 * h:256 * h + 256], T.yb[:, 256 * h:256 * h + 256])
+    store("s", a_e4, T.ev[:, :], T.e4[0:2, :])
+
+    w("g", ("sv", cnt["v"]), ("ss", cnt["s"]), ("st", cnt["t"]), ("sg", cnt["g"]), ("dout", outs[0]), ("loc", loc))

from concourse.bass import DstId, RemoteDMATransfer
from concourse.mybir import dt, AluOpType as A, AxisListType as AX, ActivationFunctionType as F

CODES, PLANE = "float8_e4m3fn_x4", "uint8"


def _f32(n):
    return ("sbuf", [128, n], "float32")


_I1 = ("sbuf", [128, 1], "int32")
SCRATCH = {
    "snd": ("dram", [128, 1], "int32"), "snr": ("sbuf", [128, 8], "int32"), "xt": ("sbuf", [128, 520], "bfloat16"),
    "ut": ("sbuf", [128, 512], "bfloat16"), "wt": ("sbuf", [128, 512], "bfloat16"),
    "xq": ("sbuf", [128, 130], CODES), "xs": ("sbuf", [128, 130], PLANE),
    "uq": ("sbuf", [128, 128], CODES), "us": ("sbuf", [128, 128], PLANE),
    "ur": ("sbuf", [128, 128], CODES), "urs": ("sbuf", [128, 128], PLANE),
    "wq": ("sbuf", [128, 128], CODES), "ws": ("sbuf", [128, 128], PLANE),
    "kq": ("sbuf", [128, 576], CODES), "kp": ("sbuf", [128, 576], PLANE),
    "pq": ("sbuf", [128, 128], CODES), "ps": ("sbuf", [128, 128], PLANE),
    "fwl": ("dram", [128, 1], "int32"), "fwq": ("sbuf", [128, 32], CODES), "fws": ("sbuf", [128, 32], PLANE),
    "land": ("dram", [8, 128, 1], "int32"), "row": ("sbuf", [128, 1024], "int32"),
    "lq": ("sbuf", [128, 128], CODES), "ls": ("sbuf", [128, 128], PLANE),
    "oq": ("sbuf", [128, 512], CODES), "op": ("sbuf", [128, 512], PLANE),
    "lst": ("sbuf", [128, 8], "uint16"), "lo": ("sbuf", [128, 2], "uint16"),
    "zo": ("sbuf", [128, 8], "uint16"), "coff": ("sbuf", [128, 4], "uint16"),
    "loff": ("sbuf", [128, 32], "uint16"), "roff": ("sbuf", [128, 16], "uint16"),
    "qall": ("sbuf", [128, 2], "uint16"), "qown": ("sbuf", [128, 2], "uint16"),
    "pi": _I1, "pm": _I1, "pm32": _I1, "ia": _I1, "ib": _I1, "ic": _I1, "id5": _I1,
    "pmf": _f32(1), "fa": _f32(1), "fx": _f32(1), "fc": _f32(1), "fd": _f32(1), "is0": _f32(1), "nm": _f32(1),
    "q16": _f32(32), "jw": _f32(32), "kb": _f32(4), "zr": _f32(128), "k64": _f32(64), "jio": _f32(128), "jrow": _f32(128),
    "c0": ("sbuf", [128, 640], "bfloat16"), "c1": ("sbuf", [128, 640], "bfloat16"),
    "c2": ("sbuf", [128, 640], "bfloat16"), "c3": ("sbuf", [128, 640], "bfloat16"),
    "junk": ("sbuf", [128, 640], "bfloat16"), "junv": ("sbuf", [128, 128], "bfloat16"),
    "tb": _f32(448), "tt": _f32(128), "rin": _f32(32), "rwp": _f32(32), "l1": _f32(32), "l2": _f32(32), "l3": _f32(32),
    "fl": _f32(128), "pin1": _f32(128), "pinc": _f32(128), "zq": _f32(4), "zv": _f32(4), "m64": _f32(64),
    "evi": _f32(128), "ev2": _f32(128), "evw": _f32(512), "ep": _f32(256), "e1": _f32(128), "e2": _f32(64), "e3": _f32(64),
    "e4": _f32(64), "yb": _f32(512),
    "pr": ("psum", [128, 512], "float32"), "pc": ("psum", [128, 2048], "float32"),
    "p2": ("psum", [128, 512], "float32"), "py": ("psum", [128, 1024], "float32"),
}
SEMAPHORES = ["sv", "ss", "st", "sg", "dsn", "dsd", "dx", "du", "dk", "dw", "down", "drow", "dr", "dev", "dout",
              "aL", "aC", "aS", "fC", "fS", "loc"]


def bits(es):
    m = 0
    for e in es:
        m |= 1 << e
    return m


def u8(v):
    return v.bitcast(dt.uint8)


def u32(v):
    return v.bitcast(dt.uint32)


def split(es, n, turn=0):
    if n == 1:
        return [es]
    h = len(es) // 2
    if n == 2:
        return [es[:h], es[h:]]
    q = h // 2
    wide, rest = (es[:h], [es[h:h + q], es[h + q:]]) if turn % 2 == 0 else (es[h:], [es[:q], es[q:h]])
    return rest[:turn] + [wide] + rest[turn:]


def plan(s, T, topo):
    core = T.cores[s]
    n = len(T.cores)
    cross = [d for d in range(n) if d != s and not topo.may_write(core, T.cores[d])]
    home = [d for d in range(n) if d not in cross]
    same = [d for d in home if d != s]
    chip = [f for f in topo.cores_of(core) if f != core]
    ports = [f for f in chip if all(topo.may_write(f, T.cores[d]) for d in cross)]
    near = [f for f in ports if topo.die(f) == topo.die(core)]
    far = [f for f in ports if topo.die(f) != topo.die(core)]
    a, b = (near, far) if (s // 2) % 2 == 0 else (far, near)
    off = topo.engines(core, T.cores[same[0]])
    on = [e for e in topo.engines(core, near[0]) if e not in off]
    h = len(on) // 2
    hop = [(k, es, f, ds) for i, k in enumerate("CS") for es, f, ds in ((on[:h], a[i], cross[:2]), (on[h:], b[i], cross[2:]))]
    straight = [(k, es, d) for i, k in enumerate("CS") for es, d in zip(split(off, 3, i), same)]
    return {"core": core, "cross": cross, "home": home, "same": same, "order": cross + home, "on": on, "off": off,
            "list": list(zip([a[0], a[1], b[0], b[1]], cross)), "hop": hop, "straight": straight}


def last_leg(f, ds, T, topo):
    return split(topo.engines(f, T.cores[ds[0]]), len(ds))


def xfer(src_core, dst_cores, es, sem, src, dsts, topo):
    ids = []
    for d in dst_cores:
        rid, pid = topo.addr(d, src_core)
        ids.append(DstId(rid=rid, pnc=pid))
    return RemoteDMATransfer(dst_ids=ids, dma_engine_mask=bits(es), remote_sem=sem, srcs=[src], dsts=dsts)


def part(T, k, codes, plane, i, n):
    return u8(T[codes][:, 16 * i:16 * (i + n)]) if k == "C" else T[plane][:, 16 * i:16 * (i + n)]


def forward(g, core, s, T, topo):
    p = plan(s, T, topo)
    loc = 0
    for f, d in p["list"]:
        if f == core:
            es = topo.engines(core, T.cores[d])[:1]
            g.wait_ge(T.sem.aL, 1)
            g.remote_dma_fused([xfer(core, [T.cores[d]], es, T.sem.aL, T.fwl[:, :], [T.land[s]], topo)], local_sem=T.sem.loc)
            loc += len(es)
    for k, es, f, ds in p["hop"]:
        if f == core:
            g.wait_ge(T.sem["f" + k], len(es))
            ts = []
            for i, (d, me) in enumerate(zip(ds, last_leg(core, ds, T, topo))):
                ts.append(xfer(core, [T.cores[d]], me, T.sem["a" + k], part(T, k, "fwq", "fws", i, 1),
                               [part(T, k, "lq", "ls", s, 1)], topo))
                loc += len(me)
            g.remote_dma_fused(ts, local_sem=T.sem.loc)
    if loc:
        g.wait_ge(T.sem.loc, loc)


def rank_program(g, core, T, topo):
    r = T.rank_of(core)
    n = len(T.cores)
    if r is None:
        for s in range(n):
            if T.cores[s] in topo.cores_of(core):
                forward(g, core, s, T, topo)
        return
    P = plan(r, T, topo)
    V, S, E, Y = g.vector, g.scalar, g.tensor, g.sync
    sem = T.sem
    queue = {"v": V, "s": S, "t": E, "g": g, "y": Y}
    cnt = {"v": 0, "s": 0, "t": 0, "g": 0}
    seen = {}

    def w(name, *tags):
        for sn, val in tags:
            if seen.get((name, sn), 0) < val:
                queue[name].wait_ge(sem[sn], val)
                seen[(name, sn)] = val

    def do(name, call, tags):
        w(name, *tags)
        call().then_inc(sem["s" + name], 1)
        cnt[name] += 1
        return ("s" + name, cnt[name])

    def v(call, *tags):
        return do("v", call, tags)

    def sc(call, *tags):
        return do("s", call, tags)

    def mm(call, *tags):
        return do("t", call, tags)

    def gg(call, *tags):
        return do("g", call, tags)

    need = {"L": n - 1, "C": 0, "S": 0}
    for s in range(n):
        if s == r:
            continue
        p = plan(s, T, topo)
        for k, es, f, ds in p["hop"]:
            if r in ds:
                need[k] += len(last_leg(f, ds, T, topo)[ds.index(r)])
        for k, es, d in p["straight"]:
            if d == r:
                need[k] += len(es)

    Y.dma_start(T.snd[:, :], T.sn[:, :]).then_inc(sem.dsd, 16)
    S.dma_start(T.xt[:, 8:520], T.x[:, :]).then_inc(sem.dx, 16)
    for k in range(8):
        (Y if k < 4 else S).dma_start(T.snr[16 * k:16 * k + 16, :], T.sn[:, :]).then_inc(sem.dsn, 16)
    Y.dma_start(T.ut[:, 0:8], T.u[:, 0:8]).then_inc(sem.du, 16)
    S.dma_start(T.kp[:, 64:576], T.ks[:, :]).then_inc(sem.dk, 16)
    Y.dma_start(u8(T.kq[:, 64:576]), T.kc[:, :]).then_inc(sem.dk, 16)
    Y.dma_start(T.wt[:, :], T.w[:, :]).then_inc(sem.dw, 16)
    Y.dma_start(T.land[r], T.sn[:, :]).then_inc(sem.down, 16)
    SN, DX, DU, DK, DW = ("dsn", 128), ("dx", 16), ("du", 16), ("dk", 32), ("dw", 16)

    a_x0 = v(lambda: V.memset(T.xt[:, 0:8], 0.0))
    a_u0 = v(lambda: V.memset(T.ut[:, 8:512], 0.0))
    a_zo = v(lambda: V.memset(T.zo[:, :], 0))
    a_pi = gg(lambda: g.iota(T.pi[:, :], [[1, 1]], 0, 1))
    a_q16 = gg(lambda: g.iota(T.q16[:, :], [[16, 32]], 0, 0, allow_small_or_imprecise_dtypes=True))
    a_jio = gg(lambda: g.iota(T.jio[:, :], [[1, 128]], 1, 4, allow_small_or_imprecise_dtypes=True))
    t1 = v(lambda: V.tensor_scalar(T.ia[:, :], T.pi[:, :], 1, 3, A.logical_shift_right, A.bitwise_and), a_pi)
    t2 = v(lambda: V.tensor_scalar(T.ib[:, :], T.pi[:, :], 1, None, A.bitwise_and))
    t3 = v(lambda: V.tensor_scalar(T.ic[:, :], T.pi[:, :], 3, 1, A.logical_shift_right, A.bitwise_and))
    t4 = v(lambda: V.tensor_scalar(T.id5[:, :], T.pi[:, :], 5, None, A.logical_shift_right))
    t1 = v(lambda: V.tensor_scalar(T.fa[:, :], T.ia[:, :], 8, None, A.mult), t1)
    t3 = v(lambda: V.tensor_scalar(T.fc[:, :], T.ic[:, :], 2, None, A.mult), t3)
    t5 = v(lambda: V.tensor_scalar(T.pm32[:, :], T.pi[:, :], 31, None, A.bitwise_and))

    cx, hm = P["cross"], P["home"]
    stx, sth = cx[1] - cx[0], hm[1] - hm[0]
    a_lx = v(lambda: V.tensor_scalar(T.lst[:, 0:4], T.snr[:, cx[0]:cx[0] + 3 * stx + 1:stx], 2, None, A.add), SN)
    a_ly = v(lambda: V.tensor_scalar(T.lst[:, 4:8], T.snr[:, hm[0]:hm[0] + 3 * sth + 1:sth], 2, None, A.add))
    a_lo = v(lambda: V.tensor_scalar(T.lo[:, 0:1], T.snr[:, r:r + 1], 2, None, A.add))
    a_xq = v(lambda: V.quantize_mx(T.xq[:, 0:130], T.xs[:, 0:130], T.xt[:, 0:520]), DX, a_x0)

    def pick(o, oc, i, ic, off, lc, vt, st):
        x = v(lambda: V.tensor_copy(u32(T[o[0]][:, oc[0]:oc[1]]), u32(T[i[0]][:, ic[0]:ic[1]]).indirect(T[off][:, lc[0]:lc[1]])), *vt)
        y = sc(lambda: S.activation(T[o[1]][:, oc[0]:oc[1]], T[i[1]][:, ic[0]:ic[1]].indirect(T[off][:, lc[0]:lc[1]]), F.Copy), *st)
        return x, y

    X, XW = ("xq", "xs"), (0, 130)
    px = pick(("pq", "ps"), (0, 64), X, XW, "lst", (0, 4), (a_xq, a_lx), (a_xq, a_lx))
    py = pick(("pq", "ps"), (64, 128), X, XW, "lst", (4, 8), (a_ly,), (a_ly,))

    loc = 0

    def send(ts, es):
        g.remote_dma_fused(ts, local_sem=sem.loc)
        return sum(len(e) for e in es)

    def hop(k):
        calls = [c for c in P["hop"] if c[0] == k]
        return send([xfer(core, [f], es, sem["f" + k], part(T, k, "pq", "ps", P["order"].index(ds[0]), 2),
                          [part(T, k, "fwq", "fws", 0, 2)], topo) for _, es, f, ds in calls], [c[1] for c in calls])

    def straight(k):
        calls = [c for c in P["straight"] if c[0] == k]
        return send([xfer(core, [T.cores[d]], es, sem["a" + k], part(T, k, "pq", "ps", P["order"].index(d), 1),
                          [part(T, k, "lq", "ls", r, 1)], topo) for _, es, d in calls], [c[1] for c in calls])

    w("g", ("dsd", 16))
    fs = [f for f, d in P["list"]]
    le = [P["on"][:1], P["off"][:1]]
    loc += send([xfer(core, fs, le[0], sem.aL, T.snd[:, :], [T.fwl[:, :] for f in fs], topo),
                 xfer(core, [T.cores[d] for d in P["same"]], le[1], sem.aL, T.snd[:, :], [T.land[r] for d in P["same"]], topo)], le)
    w("g", px[0])
    loc += hop("C")
    w("g", px[1])
    loc += hop("S")
    w("g", py[0])
    loc += straight("C")
    w("g", py[1])
    loc += straight("S")

    a_uq = v(lambda: V.quantize_mx(T.uq[:, :], T.us[:, :], T.ut[:, :]), DU, a_u0)
    ur = pick(("ur", "urs"), (0, 128), ("uq", "us"), (0, 128), "zo", (0, 8), (a_uq, a_zo), (a_uq, a_zo))
    po = pick(("lq", "ls"), (16 * r, 16 * r + 16), X, XW, "lo", (0, 1), (a_lo,), (a_lo,))
    a_row = mm(lambda: E.matmul_mx(T.pr[:, :], T.ur[:, :], T.urs[:, :], T.kq[:, 64:576], T.kp[:, 64:576], True, True), DK, *ur)
    turn = (1, 2, 3, 0)
    a_col = {}
    for c in turn:
        lo, hi = 64 + 128 * c, 192 + 128 * c
        a_col[c] = mm(lambda: E.matmul_mx(T.pc[:, 512 * c:512 * c + 128], T.kq[:, lo:hi], T.kp[:, lo:hi],
                                          T.ur[:, :], T.urs[:, :], True, True))
    a_row2 = mm(lambda: E.matmul_mx(T.p2[:, :], T.ur[:, :], T.urs[:, :], T.kq[:, 64:576], T.kp[:, 64:576], True, True))
    a_tin = v(lambda: V.memset(T.tb[:, 320:448], 0.0))
    t1 = v(lambda: V.tensor_tensor(T.fx[:, :], T.fa[:, :], T.ib[:, :], A.add), t1, t2)
    t = v(lambda: V.tensor_scalar(T.pm[:, :], T.pi[:, :], 15, None, A.bitwise_and))
    t4 = v(lambda: V.tensor_scalar(T.fd[:, :], T.id5[:, :], 2, None, A.mult), t4)
    a_pm = v(lambda: V.tensor_scalar(T.qall[:, 0:1], T.fx[:, :], T.fc[:, 0:1], None, A.add), t1, t3)
    a_pm = v(lambda: V.tensor_scalar(T.qall[:, 1:2], T.fx[:, :], T.fc[:, 0:1], 4.0, A.add, A.add))
    t = v(lambda: V.tensor_copy(T.pmf[:, :], T.pm[:, :]), t)
    a_pq = v(lambda: V.tensor_scalar(T.qown[:, 0:1], T.fx[:, :], T.fd[:, 0:1], None, A.add), t4)
    a_nm = v(lambda: V.tensor_scalar(T.nm[:, :], T.pm32[:, :], 0, None, A.is_gt), t5)
    a_is0 = v(lambda: V.tensor_scalar(T.is0[:, :], T.pm32[:, :], 0, None, A.is_equal))

    sums = []
    for c in turn:
        b = T["c%d" % c]
        sj = T.pc[:, 512 * c:512 * c + 1]
        own = T.pr[:, 128 * c:128 * c + 128]
        t0 = v(lambda: V.tensor_scalar(b[:, 512:640], own, sj, None, A.is_equal), a_row, a_col[c])
        masked = gg(lambda: g.affine_select(b[:, 512:640], b[:, 512:640], [[-1, 128]], A.is_gt, 0.0, 0, 1), t0)
        if c:
            v(lambda: V.tensor_scalar(b[:, 0:128 * c], T.pr[:, 0:128 * c], sj, None, A.is_le))
        t0 = v(lambda: V.tensor_scalar(b[:, 128 * c:512], T.pr[:, 128 * c:512], sj, None, A.is_lt))
        if c:
            sums.append(sc(lambda: S.activation(T.junk[:, :], b[:, :], F.Copy, accum_out=T.tb[:, 320 + 32 * c:321 + 32 * c]),
                           t0, masked, a_tin, *sums[-1:]))
        else:
            sums.append(v(lambda: V.tensor_tensor_scan(T.tb[:, 1:321], b[:, 0:320], b[:, 320:640], 0.0, A.add, A.add),
                          t0, masked, a_tin))
    a_k64 = gg(lambda: g.iota(T.k64[:, :], [[1, 64]], 0, 0, allow_small_or_imprecise_dtypes=True))
    w("y", ("aL", need["L"]), ("down", 16))
    Y.dma_start(T.row[0:1, :], T.land[:, :, :]).then_inc(sem.drow, 16)
    a_tt = v(lambda: V.transpose(T.tt[:, :], T.tb[:, 320:448]), *sums)
    for a in range(4):
        nm = "sy"[a % 2]
        w(nm, a_tt)
        queue[nm].dma_start(T.rin[32 * a:32 * a + 32, 0:16], T.tt[0:128:32, :]).then_inc(sem.dr, 16)
    a_kb = v(lambda: V.tensor_scalar(T.kb[:, :], T.q16[:, 0:4], T.pmf[:, 0:1], 0.5, A.add, A.add), t, a_q16)
    a_jw = v(lambda: V.tensor_scalar(T.jw[:, :], T.q16[:, :], T.pmf[:, 0:1], 64.0, A.add, A.add))
    a_zr = v(lambda: V.memset(T.zr[0:1, :], 0.0))
    for a in range(4):
        a_evi = sc(lambda: S.activation(T.evi[32 * a:32 * a + 32, :], T.p2[32 * a:32 * a + 32, 128 * a:128 * a + 128], F.Identity,
                                        scale=T.nm[32 * a:32 * a + 32, 0:1]), a_row2, a_nm)
    a_wq = v(lambda: V.quantize_mx(T.wq[:, :], T.ws[:, :], T.wt[:, :]), DW)

    t = v(lambda: V.tensor_scalar(T.fl[0:1, :], T.row[0:1, r:1024:8], 0, None, A.is_ge), ("drow", 16))
    t = v(lambda: V.tensor_tensor_scan(T.pin1[0:1, :], T.fl[0:1, :], T.zr[0:1, :], 0.0, A.add, A.add), t, a_zr)
    a_pinc = gg(lambda: g.partition_broadcast(T.pinc[:, :], T.pin1[0:1, :], 128), t)
    m = T.pinc[:, 127:128]
    a_z = sums[2]
    for q in range(3):
        a_z = sc(lambda: S.activation(T.junk[:, 0:127], T.pinc[:, 0:127], F.Sign, bias=T.kb[:, q:q + 1], scale=-1.0,
                                      accum_out=T.zq[:, q:q + 1]), a_pinc, a_kb, a_z)
    a_jr = v(lambda: V.tensor_scalar(T.jrow[:, :], T.jio[:, :], T.is0[:, 0:1], None, A.mult), a_jio, a_is0)
    a_w0 = v(lambda: V.memset(T.evw[:, 0:64], 0.0))
    a_ev2 = v(lambda: V.tensor_tensor(T.ev2[:, :], T.evi[:, :], T.jrow[:, :], A.add), a_evi, a_jr)
    t1 = v(lambda: V.tensor_scalar(T.junv[:, 0:127], T.pinc[:, 0:127], T.kb[:, 3:4], None, A.is_le), a_pinc)
    a_m64 = v(lambda: V.tensor_scalar(T.m64[0:2, :], T.k64[0:2, :], T.pinc[0:2, 127:128], None, A.is_lt), a_k64)
    t1 = v(lambda: V.tensor_reduce(T.zv[:, 0:1], T.junv[:, 0:127], AX.X, A.add), t1)
    t = v(lambda: V.tensor_copy(T.rin[:, 16:32], T.rin[:, 0:16]), ("dr", 64))
    a_c3 = v(lambda: V.tensor_copy(T.coff[:, 3:4], T.zv[:, 0:1]), t1)
    a_rwp = v(lambda: V.transpose(T.rwp[:, :], T.rin[:, :]), t)
    t = v(lambda: V.tensor_scalar(T.l1[:, :], T.rwp[:, :].indirect(T.qall[:, 0:2]), m, 2048.0, A.is_ge, A.mult), a_rwp, a_pm)
    a_roff = v(lambda: V.tensor_copy(T.roff[:, :], T.rwp[:, :].indirect(T.qown[:, 0:1])), a_pq)
    t = v(lambda: V.tensor_tensor(T.l2[:, :], T.rwp[:, :].indirect(T.qall[:, 0:2]), T.l1[:, :], A.max), t)
    t = v(lambda: V.tensor_tensor(T.l3[:, :], T.l2[:, :], T.jw[:, :], A.min), t, a_jw)
    a_ev = v(lambda: V.tensor_copy(T.evw[:, 0:512].indirect(T.roff[:, 0:8]), T.ev2[:, :]), a_roff, a_ev2, a_w0)
    a_loff = v(lambda: V.tensor_copy(T.loff[:, :], T.l3[:, :]), t)
    a_coff = v(lambda: V.tensor_scalar(T.coff[:, 0:3], T.zq[:, 0:3], 0.5, 63.5, A.mult, A.add), a_z)
    w("y", a_ev)
    for i in range(2):
        Y.dma_start(T.ep[i:i + 1, :], T.evw[i:128:32, 0:64]).then_inc(sem.dev, 16)

    cc, cs = pick(("kq", "kp"), (0, 64), ("lq", "ls"), (0, 128), "coff", (0, 4),
                  (("aC", need["C"]), po[0], a_coff, a_c3), (("aS", need["S"]), po[1], a_coff, a_c3))
    fin = []
    for h in range(2):
        fin.append(pick(("oq", "op"), (256 * h, 256 * h + 256), ("kq", "kp"), (0, 576), "loff", (16 * h, 16 * h + 16),
                        (cc, a_loff), (cs, a_loff)))
    yc = []
    for h in range(2):
        lo, hi = 256 * h, 256 * h + 256
        ym = mm(lambda: E.matmul_mx(T.py[:, 512 * h:512 * h + 256], T.wq[:, :], T.ws[:, :], T.oq[:, lo:hi], T.op[:, lo:hi],
                                    True, True), a_wq, *fin[h])
        yc.append(v(lambda: V.tensor_copy(T.yb[:, lo:hi], T.py[:, 512 * h:512 * h + 256]), ym))
    t = v(lambda: V.tensor_tensor(T.e1[0:2, :], T.ep[0:2, 0:128], T.ep[0:2, 128:256], A.add), ("dev", 32))
    t = v(lambda: V.tensor_tensor(T.e2[0:2, :], T.e1[0:2, 0:64], T.e1[0:2, 64:128], A.add), t)
    t = v(lambda: V.tensor_tensor(T.e3[0:2, :], T.e2[0:2, :], T.m64[0:2, :], A.mult), t, a_m64)
    a_e4 = v(lambda: V.tensor_scalar(T.e4[0:2, :], T.e3[0:2, :], T.is0[0:2, 0:1], None, A.subtract), t)

    outs = [0]

    def store(nm, tag, o, i):
        w(nm, tag)
        queue[nm].dma_start(o, i).then_inc(sem.dout, 16)
        outs[0] += 16

    for h in range(2):
        store("y", fin[h][0], T.oc[:, 1024 * h:1024 * h + 1024], u8(T.oq[:, 256 * h:256 * h + 256]))
    for k in range(4):
        store("s", fin[1][1], T.osc[4 * k:4 * k + 4, :], T.op[32 * k:32 * k + 4, :])
    for h in range(2):
        store("y", yc[h], T.y[:, 256 * h:256 * h + 256], T.yb[:, 256 * h:256 * h + 256])
    store("s", a_e4, T.ev[:, :], T.e4[0:2, :])

    w("g", ("sv", cnt["v"]), ("ss", cnt["s"]), ("st", cnt["t"]), ("sg", cnt["g"]), ("dout", outs[0]), ("loc", loc))
